import numpy as np
import ml_dtypes


def mxq(x, axis, fmt="e4m3"):
    dtype, down = {"e4m3": (ml_dtypes.float8_e4m3fn, 7), "e5m2": (ml_dtypes.float8_e5m2, 14)}[fmt]
    v = np.moveaxis(np.asarray(x, np.float32).astype(ml_dtypes.bfloat16).astype(np.float64), axis, -1)
    blocks = v.reshape(v.shape[:-1] + (-1, 32))
    amax = np.abs(blocks).max(-1, keepdims=True)
    byte = np.maximum(np.where(amax > 0, np.frexp(amax)[1] - 1 + 127, 0) - down, 1)
    scale = np.exp2(byte - 127.0)
    codes = (blocks / scale).astype(np.float32).astype(dtype).astype(np.float64)
    return np.moveaxis((codes * scale).reshape(v.shape), -1, axis)


WIDE = False


def mx_kscale(k):
    if not WIDE:
        return np.ones(k)
    levels = np.array([10, -10, 5, -5, 0])
    if k % 512:
        return np.exp2(np.random.permutation(np.resize(levels, k // 32))).repeat(32)
    a = np.empty((k // 512, 16))
    for p in range(k // 512):
        a[p, :8] = np.random.permutation(np.resize(levels, 8))
        for g in range(8):
            far = levels[np.abs(levels - a[p, g]) >= 10]
            a[p, g + 8] = far[np.random.randint(len(far))]
    return np.exp2(a.ravel()).repeat(32)


def f64(x):
    return np.asarray(x).astype(np.float64)


def striped(idx):
    return np.tile(idx.reshape(-1, 16).T, (8, 1)).astype(np.uint16)


def unstriped(offs):
    return offs[:16].T.reshape(-1).astype(np.int64)


E2M1 = np.array([0.0, 0.5, 1.0, 1.5, 2.0, 3.0, 4.0, 6.0, -0.0, -0.5, -1.0, -1.5, -2.0, -3.0, -4.0, -6.0])


def pack_weight(w, fmt):
    k, n = w.shape
    w = f64(np.asarray(w, np.float32).astype(ml_dtypes.bfloat16)).reshape(k // 32, 32, n)
    amax = np.abs(w).max(1)
    if fmt == "e4m3":
        byte = np.frexp(amax)[1] - 1 + 127 - 7
    else:
        mant, ex = np.frexp(amax / 6.0)
        byte = np.where(mant > 0.5, ex, ex - 1) + 127
    byte = np.clip(np.where(amax > 0, byte, 1), 1, 254)
    scaled = (w * np.exp2(127.0 - byte)[:, None, :]).reshape(k, n).astype(np.float32)
    by_word = np.ascontiguousarray(scaled.reshape(k // 512, 128, 4, n).transpose(0, 1, 3, 2))
    if fmt == "e4m3":
        words = by_word.astype(ml_dtypes.float8_e4m3fn).view(np.uint8)
    else:
        c = by_word.astype(ml_dtypes.float4_e2m1fn).view(np.uint8) & 0xF
        words = (c[..., 0::2] | (c[..., 1::2] << 4)).reshape(k // 512, 128, 2 * n)
    return np.ascontiguousarray(words), np.ascontiguousarray(byte.astype(np.uint8).reshape(k // 512, 16, n))


def unpack_weight(words, scales, fmt):
    g, _, n = scales.shape
    words = np.ascontiguousarray(words).reshape(g, 128, n, -1)
    if fmt == "e4m3":
        vals = words.view(ml_dtypes.float8_e4m3fn).astype(np.float64)
    else:
        nib = np.empty((g, 128, n, 4), np.uint8)
        nib[..., 0::2] = words & 0xF
        nib[..., 1::2] = words >> 4
        vals = E2M1[nib]
    vals = vals * np.repeat(np.exp2(scales.astype(np.float64) - 127.0), 8, axis=1)[..., None]
    return vals.transpose(0, 1, 3, 2).reshape(g * 512, n)


def gelu(v):
    return 0.5 * v * (1.0 + np.tanh(np.sqrt(2.0 / np.pi) * (v + 0.044715 * v**3)))


def bf(x):
    return np.asarray(x, np.float32).astype(ml_dtypes.bfloat16)


def planes(Y):
    n, m = Y.shape
    b = f64(bf(Y)).reshape(n // 32, 32, m)
    amax = np.abs(b).max(1)
    byte = np.clip(np.where(amax > 0, np.frexp(amax)[1] - 1 + 127 - 7, 1), 1, 254)
    codes = (b * np.exp2(127.0 - byte)[:, None, :]).reshape(n, m).astype(np.float32).astype(ml_dtypes.float8_e4m3fn).view(np.uint8)
    words = codes.reshape(n // 512, 128, 4, m).transpose(0, 1, 3, 2)
    return np.ascontiguousarray(words), np.ascontiguousarray(byte.astype(np.uint8).reshape(n // 512, 16, m))


K, T, S, H, M, N, P = 512, 2048, 1024, 1024, 512, 512, 512

def setup_inputs():
    n = np.random.standard_normal
    s = mx_kscale(K)[:, None]
    u = mx_kscale(H)[:, None]
    u2 = mx_kscale(M)[:, None]
    tab_words, tab_scales = pack_weight(n((K, T)) * s, "e4m3")
    w2_words, w2_scales = pack_weight(1.8 * n((K, M)) / np.sqrt(K) / s, "e2m1")
    wc_words, wc_scales = pack_weight(0.6 * n((H, N)) / np.sqrt(H) / u, "e4m3")
    return {
        "tab_words": tab_words, "tab_scales": tab_scales,
        "offs": striped(np.random.permutation(T)[:S]),
        "pos1": striped(np.random.permutation(S)[:P]),
        "pos2": striped(np.random.permutation(S)[:P]),
        "w1": (n((K, H)) / np.sqrt(K) / s * u.T).astype(np.float32),
        "b1": (0.5 * n(H) * u[:, 0]).astype(np.float32),
        "w2_words": w2_words, "w2_scales": w2_scales,
        "qgain": (np.random.uniform(0.6, 1.6, M) * u2[:, 0]).astype(np.float32),
        "wa": (0.4 * n((H, N)) / np.sqrt(H) / u).astype(np.float32),
        "wb": (0.85 * n((M, N)) / np.sqrt(M) / u2).astype(np.float32),
        "wc_words": wc_words, "wc_scales": wc_scales,
        "steep": np.random.uniform(1, 3, N).astype(np.float32),
        "share": np.random.uniform(0.1, 0.5, N).astype(np.float32),
        "mat": (2.0 * n((N, P))).astype(np.float32),
        "gain": np.exp(0.8 * n(N)).astype(np.float32),
    }

def reference(tab_words, tab_scales, offs, pos1, pos2, w1, b1, w2_words, w2_scales, qgain, wa, wb,
              wc_words, wc_scales, steep, share, mat, gain):
    v = unpack_weight(tab_words, tab_scales, "e4m3")[:, unstriped(offs)]
    w2 = unpack_weight(w2_words, w2_scales, "e2m1")
    wc = unpack_weight(wc_words, wc_scales, "e4m3")
    h = (mxq(f64(w1), 0, "e4m3").T @ v) + f64(b1)[:, None]
    q = np.tanh(w2.T @ v) * f64(qgain)[:, None]
    hq = mxq(h, 0, "e4m3")
    qq = mxq(q, 0, "e4m3")
    e = mxq(f64(wa), 0, "e4m3").T @ hq + mxq(f64(wb), 0, "e4m3").T @ qq
    d = wc.T @ hq
    top = e.max(axis=1)
    a = 1.0 / (1.0 + np.exp(-f64(steep)[:, None] * (e[:, unstriped(pos1)] - f64(share)[:, None] * top[:, None])))
    y = f64(gain)[:, None] * (f64(mat) * a + d[:, unstriped(pos2)])
    words, scales = planes(y)
    return y, words, scales

@@ -1,0 +1,299 @@
+from contextlib import ExitStack
+
+import concourse.mybir as mybir
+
+K, T, S, H, M, N, PICKS = 512, 2048, 1024, 1024, 512, 512, 512
+FLOPS = 2 * S * (K * H + K * M + H * N + M * N + H * N)
+
+F32 = mybir.dt.float32
+BF16 = mybir.dt.bfloat16
+I32 = mybir.dt.int32
+U32 = mybir.dt.uint32
+U16 = mybir.dt.uint16
+U8 = mybir.dt.uint8
+FP8X4 = mybir.dt.float8_e4m3fn_x4
+FP4X4 = mybir.dt.float4_e2m1fn_x4
+ACT = mybir.ActivationFunctionType
+ALU = mybir.AluOpType
+
+P = 128
+PACK = 4
+GROUP = P * PACK
+HALF = 512
+CHUNK = 128
+QUADS = 4
+
+
+def tile_list_gust_front_page_kernel(
+    tc, tab_words, tab_scales, offs, pos1, pos2, w1, b1, w2_words, w2_scales, qgain, wa, wb,
+    wc_words, wc_scales, steep, share, mat, gain, out_0, out_1, out_2,
+):
+    nc = tc.nc
+    with ExitStack() as ctx:
+        keep = ctx.enter_context(tc.tile_pool(name="keep", bufs=1))
+        psum = ctx.enter_context(tc.psum_pool(name="psum", bufs=8))
+
+        def sb(shape, dtype, name):
+            return keep.tile(shape, dtype, name=name, align_bytes=64)
+
+        def bank():
+            return psum.tile([P, 512], F32, name="bank")
+
+        offs_sb = keep.tile([P, S // 16], U16, name="offs_sb")
+        pos1_sb = keep.tile([P, PICKS // 16], U16, name="pos1_sb")
+        pos2_sb = keep.tile([P, PICKS // 16], U16, name="pos2_sb")
+
+        tab_w = sb([P, T], I32, "tab_w")
+        tab_s = sb([P, T], U8, "tab_s")
+        w2_raw = sb([P, 2 * M], U8, "w2_raw")
+        w2_sraw = sb([P, M], U8, "w2_sraw")
+        wc_raw = sb([P, 2 * N], I32, "wc_raw")
+        wc_sraw = sb([P, N], U8, "wc_sraw")
+        w1_raw = [sb([P, PACK, 256], F32, "w1_raw%d" % i) for i in range(4)]
+        wa_raw = [sb([P, PACK, N], F32, "wa_raw%d" % a) for a in range(2)]
+        wb_raw = sb([P, PACK, N], F32, "wb_raw")
+        mat_sb = sb([P, PACK, PICKS], F32, "mat_sb")
+        b1_sb = sb([P, 2, PACK], F32, "b1_sb")
+        qgain_sb = sb([P, PACK], F32, "qgain_sb")
+        steep_sb = sb([P, PACK], F32, "steep_sb")
+        share_sb = sb([P, PACK], F32, "share_sb")
+        gain_sb = sb([P, PACK], F32, "gain_sb")
+
+        nc.gpsimd.memset(tab_s[:].bitcast(I32), 0)
+        nc.gpsimd.memset(w2_sraw[:].bitcast(I32), 0)
+        nc.gpsimd.memset(wc_sraw[:].bitcast(I32), 0)
+
+        def load_vector(vec_sb, vec):
+            nc.sync.dma_start(out=vec_sb[:], in_=vec.rearrange("(p t) -> p t", t=PACK))
+
+        w1_rows = w1.rearrange("(p j) c -> p j c", j=PACK)
+        nc.sync.dma_start(out=tab_w[:], in_=tab_words[0].rearrange("p t i -> p (t i)").bitcast(I32))
+        nc.sync.dma_start(offs_sb[:], offs)
+        for q in range(QUADS):
+            nc.sync.dma_start(out=tab_s[32 * q : 32 * q + 4, :].bitcast(I32), in_=tab_scales[0, 4 * q : 4 * q + 4, :].bitcast(I32))
+        for i in range(2):
+            nc.sync.dma_start(out=w1_raw[i][:], in_=w1_rows[:, :, 256 * i : 256 * (i + 1)])
+        nc.sync.dma_start(out=w2_raw[:].bitcast(I32), in_=w2_words[0].bitcast(I32))
+        for q in range(QUADS):
+            nc.sync.dma_start(out=w2_sraw[32 * q : 32 * q + 4, :].bitcast(I32), in_=w2_scales[0, 4 * q : 4 * q + 4, :].bitcast(I32))
+        nc.sync.dma_start(out=b1_sb[:], in_=b1.rearrange("(g p t) -> p g t", g=2, t=PACK))
+        for i in range(2, 4):
+            nc.sync.dma_start(out=w1_raw[i][:], in_=w1_rows[:, :, 256 * i : 256 * (i + 1)])
+        load_vector(qgain_sb, qgain)
+        nc.sync.dma_start(out=wc_raw[:].rearrange("p (a c) -> p a c", a=2), in_=wc_words.rearrange("a p c i -> p a (c i)").bitcast(I32))
+        for a in range(2):
+            nc.sync.dma_start(out=wa_raw[a][:], in_=wa[GROUP * a : GROUP * (a + 1), :].rearrange("(p j) c -> p j c", j=PACK))
+        for q in range(QUADS):
+            nc.sync.dma_start(out=wc_sraw[32 * q : 32 * q + 8, :].bitcast(I32), in_=wc_scales[:, 4 * q : 4 * q + 4, :].bitcast(I32))
+        nc.sync.dma_start(out=wb_raw[:], in_=wb.rearrange("(p j) c -> p j c", j=PACK))
+        nc.sync.dma_start(out=mat_sb[:], in_=mat.rearrange("(p t) c -> p t c", t=PACK))
+        nc.sync.dma_start(pos1_sb[:], pos1)
+        nc.sync.dma_start(pos2_sb[:], pos2)
+        for vec_sb, vec in ((steep_sb, steep), (share_sb, share), (gain_sb, gain)):
+            load_vector(vec_sb, vec)
+
+        w2_w = sb([P, 2 * M], U8, "w2_w")
+        w2_s = sb([P, M], U8, "w2_s")
+
+        v_w = [sb([P, HALF], U32, "v_w%d" % h) for h in range(2)]
+        v_s = [sb([P, HALF], U8, "v_s%d" % h) for h in range(2)]
+        for h in range(2):
+            picks = offs_sb[:, h * HALF // 16 : (h + 1) * HALF // 16]
+            nc.vector.tensor_copy(v_w[h][:], tab_w[:].bitcast(U32).indirect(picks))
+            nc.vector.tensor_copy(v_s[h][:], tab_s[:].indirect(picks))
+
+        nc.scalar.copy(out=w2_w[:].bitcast(U16).rearrange("p (t m) -> p m t", t=PACK), in_=w2_raw[:].bitcast(U16).rearrange("p (m t) -> p m t", t=PACK))
+        nc.vector.tensor_copy(out=w2_s[:].rearrange("p (t m) -> p m t", t=PACK), in_=w2_sraw[:].rearrange("p (m t) -> p m t", t=PACK))
+
+        def cast_dealt(dst, raw, m0, m1):
+            out = dst[:].rearrange("p (t m j) -> p m j t", t=PACK, j=PACK)[:, m0:m1]
+            nc.scalar.copy(out=out, in_=raw.rearrange("p j (m t) -> p m j t", t=PACK))
+
+        def quantised(name):
+            return sb([P, 512], U32, name + "_w"), sb([P, 512], U8, name + "_s")
+
+        def quantise(dst, src):
+            nc.vector.quantize_mx(out=dst[0][:].bitcast(FP8X4), scales=dst[1][:], in_=src[:])
+
+        w1_bf = [sb([P, PACK * GROUP], BF16, "w1_bf%d" % g) for g in range(2)]
+        wa_bf = [sb([P, PACK * GROUP], BF16, "wa_bf%d" % a) for a in range(2)]
+        wb_bf = sb([P, PACK * GROUP], BF16, "wb_bf")
+        w1_q = [quantised("w1_q%d" % g) for g in range(2)]
+        wa_q = [quantised("wa_q%d" % a) for a in range(2)]
+        wb_q = quantised("wb_q")
+        h_bf = [[sb([P, PACK * HALF], BF16, "h_bf%d%d" % (g, h)) for h in range(2)] for g in range(2)]
+        h_q = [[quantised("h_q%d%d" % (g, h)) for h in range(2)] for g in range(2)]
+        tanh_sb = [sb([P, PACK * HALF], F32, "tanh%d" % h) for h in range(2)]
+        q_bf = [sb([P, PACK * HALF], BF16, "q_bf%d" % h) for h in range(2)]
+        q_q = [quantised("q_q%d" % h) for h in range(2)]
+        wc_w = sb([P, 2 * N], U32, "wc_w")
+        wc_s = sb([P, N], U8, "wc_s")
+        e_sb = [sb([P, S], F32, "e%d" % t) for t in range(PACK)]
+        d_sb = [sb([P, S], F32, "d%d" % t) for t in range(PACK)]
+        top0 = sb([P, PACK], F32, "top0")
+        top = sb([P, PACK], F32, "top")
+        slope = sb([P, PACK], F32, "slope")
+        bias = sb([P, PACK], F32, "bias")
+
+        def first_stage(words, scales, h, c):
+            acc = bank()
+            cols = slice(c * CHUNK, (c + 1) * CHUNK)
+            for t in range(PACK):
+                nc.tensor.matmul_mx(
+                    out=acc[:, t * CHUNK : (t + 1) * CHUNK], lhsT=words(t), lhsT_scale=scales[:, t * P : (t + 1) * P],
+                    rhs=v_w[h][:, cols].bitcast(FP8X4), rhs_scale=v_s[h][:, cols], start=True, stop=True,
+                )
+            return acc[:].rearrange("p (t n) -> p n t", t=PACK)
+
+        def woven(tile, c):
+            return tile[:, c * GROUP : (c + 1) * GROUP].rearrange("p (n t) -> p n t", t=PACK)
+
+        def spread(row):
+            return row.unsqueeze(1).to_broadcast([P, CHUNK, PACK])
+
+        def make_tanh(h):
+            for c in range(HALF // CHUNK):
+                acc = first_stage(lambda t: w2_w[:, 2 * P * t : 2 * P * (t + 1)].bitcast(FP4X4), w2_s, h, c)
+                nc.scalar.activation(out=woven(tanh_sb[h], c), in_=acc, func=ACT.Tanh)
+
+        def make_q(h):
+            nc.vector.tensor_tensor(
+                out=q_bf[h][:].rearrange("p (n t) -> p n t", t=PACK), in0=tanh_sb[h][:].rearrange("p (n t) -> p n t", t=PACK),
+                in1=qgain_sb[:].unsqueeze(1).to_broadcast([P, HALF, PACK]), op=ALU.mult,
+            )
+
+        def make_h(g, h):
+            for c in range(HALF // CHUNK):
+                acc = first_stage(lambda t: w1_q[g][0][:, P * t : P * (t + 1)].bitcast(FP8X4), w1_q[g][1], h, c)
+                nc.vector.tensor_tensor(out=woven(h_bf[g][h], c), in0=acc, in1=spread(b1_sb[:, g, :]), op=ALU.add)
+
+        def second_pass(acc, words, scales, moving, start, stop):
+            nc.tensor.matmul_mx(
+                out=acc[:], lhsT=words.bitcast(FP8X4), lhsT_scale=scales,
+                rhs=moving[0][:].bitcast(FP8X4), rhs_scale=moving[1][:], start=start, stop=stop,
+            )
+
+        def make_d(h):
+            for t in range(PACK):
+                acc = bank()
+                for a in range(2):
+                    second_pass(acc, wc_w[:, a * N + t * P : a * N + (t + 1) * P], wc_s[4 * a :, t * P : (t + 1) * P], h_q[a][h], a == 0, a == 1)
+                nc.scalar.copy(out=d_sb[t][:, h * HALF : (h + 1) * HALF], in_=acc[:])
+
+        def open_e(h):
+            accs = [bank() for t in range(PACK)]
+            for t in range(PACK):
+                cols = slice(t * P, (t + 1) * P)
+                for a in range(2):
+                    second_pass(accs[t], wa_q[a][0][:, cols], wa_q[a][1][:, cols], h_q[a][h], a == 0, False)
+            return accs
+
+        def close_e(accs, h):
+            for t in range(PACK):
+                cols = slice(t * P, (t + 1) * P)
+                second_pass(accs[t], wb_q[0][:, cols], wb_q[1][:, cols], q_q[h], False, True)
+
+        def empty_e(accs, h, t):
+            col = slice(t, t + 1)
+            nc.vector.tensor_scalar(
+                out=e_sb[t][:, h * HALF : (h + 1) * HALF], in0=accs[t][:], scalar1=1.0,
+                scalar2=(None if h == 0 else top0[:, col]), op0=ALU.mult, op1=ALU.max,
+                accum_out=(top0 if h == 0 else top)[:, col],
+            )
+
+        cast_dealt(w1_bf[0], w1_raw[0][:], 0, 64)
+        cast_dealt(w1_bf[0], w1_raw[1][:], 64, 128)
+        quantise(w1_q[0], w1_bf[0])
+        make_h(0, 0)
+        make_tanh(0)
+        cast_dealt(w1_bf[1], w1_raw[2][:], 0, 64)
+        cast_dealt(w1_bf[1], w1_raw[3][:], 64, 128)
+        make_q(0)
+        quantise(h_q[0][0], h_bf[0][0])
+        quantise(w1_q[1], w1_bf[1])
+        quantise(q_q[0], q_bf[0])
+        make_h(1, 0)
+        for a in range(2):
+            nc.scalar.copy(
+                out=wc_w[:, a * N : (a + 1) * N].rearrange("p (t m) -> p m t", t=PACK),
+                in_=wc_raw[:, a * N : (a + 1) * N].bitcast(U32).rearrange("p (m t) -> p m t", t=PACK),
+            )
+        nc.vector.tensor_copy(out=wc_s[:].rearrange("p (t m) -> p m t", t=PACK), in_=wc_sraw[:].rearrange("p (m t) -> p m t", t=PACK))
+        quantise(h_q[1][0], h_bf[1][0])
+        for a in range(2):
+            for i in range(2):
+                cast_dealt(wa_bf[a], wa_raw[a][:, :, 256 * i : 256 * (i + 1)], 64 * i, 64 * (i + 1))
+        make_h(0, 1)
+        quantise(wa_q[0], wa_bf[0])
+        quantise(h_q[0][1], h_bf[0][1])
+        for i in range(2):
+            cast_dealt(wb_bf, wb_raw[:, :, 256 * i : 256 * (i + 1)], 64 * i, 64 * (i + 1))
+        make_tanh(1)
+        make_h(1, 1)
+        quantise(wa_q[1], wa_bf[1])
+        quantise(h_q[1][1], h_bf[1][1])
+        quantise(wb_q, wb_bf)
+        make_d(0)
+        e0 = open_e(0)
+        close_e(e0, 0)
+        make_q(1)
+        nc.vector.scalar_tensor_tensor(out=slope[:], in0=steep_sb[:], scalar=-1.0, in1=share_sb[:], op0=ALU.mult, op1=ALU.mult)
+        quantise(q_q[1], q_bf[1])
+        make_d(1)
+        for t in range(PACK):
+            empty_e(e0, 0, t)
+        e1 = open_e(1)
+        close_e(e1, 1)
+
+        PART = PICKS // 2
+        gate = [sb([P, PACK, PART], F32, "gate%d" % c) for c in range(2)]
+        summed = [sb([P, PACK, PART], F32, "summed%d" % c) for c in range(2)]
+        y = [sb([P, PACK, PART], F32, "y%d" % c) for c in range(2)]
+        y_bf = [sb([P, PACK * PART], BF16, "y_bf%d" % c) for c in range(2)]
+        y_w = [sb([P, PART], U32, "y_w%d" % c) for c in range(2)]
+        y_s = sb([P, PICKS], U8, "y_s")
+        out_rows = out_0.rearrange("(p t) c -> p t c", t=PACK)
+        out_words = out_1[0].rearrange("p m t -> p (m t)").bitcast(I32)
+
+        def look(t, c):
+            col = slice(t, t + 1)
+            picks = pos1_sb[:, c * PART // 16 : (c + 1) * PART // 16]
+            nc.scalar.activation(out=gate[c][:, t, :], in_=e_sb[t][:].indirect(picks), func=ACT.Sigmoid, bias=bias[:, col], scale=steep_sb[:, col])
+
+        def combine(pair, c):
+            rows = slice(2 * pair, 2 * pair + 2)
+            cols = slice(c * PART, (c + 1) * PART)
+            picks = pos2_sb[:, c * PART // 16 : (c + 1) * PART // 16]
+            nc.vector.tensor_tensor(out=gate[c][:, rows, :], in0=gate[c][:, rows, :], in1=mat_sb[:, rows, cols], op=ALU.mult)
+            for t in range(2 * pair, 2 * pair + 2):
+                nc.vector.tensor_tensor(out=summed[c][:, t, :], in0=d_sb[t][:].indirect(picks), in1=gate[c][:, t, :], op=ALU.add)
+            for t in range(2 * pair, 2 * pair + 2):
+                nc.scalar.activation(out=y[c][:, t, :], in_=summed[c][:, t, :], func=ACT.Copy, scale=gain_sb[:, t : t + 1])
+            nc.sync.dma_start(out=out_rows[:, rows, cols], in_=y[c][:, rows, :])
+
+        def planes(c, split):
+            cols = slice(c * PART, (c + 1) * PART)
+            woven_y = y_bf[c][:].rearrange("p (c i t) -> p c t i", i=4, t=PACK)
+            rows_y = y[c][:].rearrange("p t (c i) -> p c t i", i=4)
+            if split:
+                nc.vector.tensor_copy(out=woven_y[:, :split], in_=rows_y[:, :split])
+            nc.scalar.copy(out=woven_y[:, split:], in_=rows_y[:, split:])
+            nc.vector.quantize_mx(out=y_w[c][:].bitcast(FP8X4), scales=y_s[:, cols], in_=y_bf[c][:])
+            nc.sync.dma_start(out=out_words[:, cols], in_=y_w[c][:].bitcast(I32))
+
+        for t in range(PACK):
+            col = slice(t, t + 1)
+            empty_e(e1, 1, t)
+            nc.vector.tensor_tensor(out=bias[:, col], in0=top[:, col], in1=slope[:, col], op=ALU.mult)
+            look(t, 0)
+        for t in range(PACK):
+            look(t, 1)
+        combine(0, 0)
+        combine(1, 0)
+        combine(0, 1)
+        planes(0, 0)
+        combine(1, 1)
+        planes(1, 42)
+        for q in range(QUADS):
+            queue = nc.scalar if q % 2 else nc.sync
+            queue.dma_start(out=out_2[0, 4 * q : 4 * q + 4, :].bitcast(I32), in_=y_s[32 * q : 32 * q + 4, :].bitcast(I32))

@@ -76,11 +76,11 @@ def tile_list_gust_front_page_kernel(
         nc.sync.dma_start(out=w2_raw[:].bitcast(I32), in_=w2_words[0].bitcast(I32))
         for q in range(QUADS):
             nc.sync.dma_start(out=w2_sraw[32 * q : 32 * q + 4, :].bitcast(I32), in_=w2_scales[0, 4 * q : 4 * q + 4, :].bitcast(I32))
-        nc.sync.dma_start(out=b1_sb[:], in_=b1.rearrange("(g p t) -> p g t", g=2, t=PACK))
-        for i in range(2, 4):
-            nc.sync.dma_start(out=w1_raw[i][:], in_=w1_rows[:, :, 256 * i : 256 * (i + 1)])
-        load_vector(qgain_sb, qgain)
         nc.sync.dma_start(out=wc_raw[:].rearrange("p (a c) -> p a c", a=2), in_=wc_words.rearrange("a p c i -> p a (c i)").bitcast(I32))
+        nc.sync.dma_start(out=w1_raw[2][:], in_=w1_rows[:, :, 512:768])
+        nc.sync.dma_start(out=b1_sb[:], in_=b1.rearrange("(g p t) -> p g t", g=2, t=PACK))
+        load_vector(qgain_sb, qgain)
+        nc.sync.dma_start(out=w1_raw[3][:], in_=w1_rows[:, :, 768:1024])
         for a in range(2):
             nc.sync.dma_start(out=wa_raw[a][:], in_=wa[GROUP * a : GROUP * (a + 1), :].rearrange("(p j) c -> p j c", j=PACK))
         for q in range(QUADS):
@@ -96,18 +96,48 @@ def tile_list_gust_front_page_kernel(
         w2_s = sb([P, M], U8, "w2_s")
 
         v_w = [sb([P, HALF], U32, "v_w%d" % h) for h in range(2)]
-        v_s = [sb([P, HALF], U8, "v_s%d" % h) for h in range(2)]
-        for h in range(2):
-            picks = offs_sb[:, h * HALF // 16 : (h + 1) * HALF // 16]
-            nc.vector.tensor_copy(v_w[h][:], tab_w[:].bitcast(U32).indirect(picks))
-            nc.vector.tensor_copy(v_s[h][:], tab_s[:].indirect(picks))
+        v_s = [sb([P, HALF], U8, "v_s0")]
+
+        def gather_words(h):
+            nc.vector.tensor_copy(v_w[h][:], tab_w[:].bitcast(U32).indirect(offs_sb[:, h * HALF // 16 : (h + 1) * HALF // 16]))
+
+        def gather_scales(h):
+            if h:
+                v_s.append(keep.tile([P, HALF], U8, name="v_s1", tag="w1_bf0", align_bytes=64))
+            nc.vector.tensor_copy(v_s[h][:], tab_s[:].indirect(offs_sb[:, h * HALF // 16 : (h + 1) * HALF // 16]))
+
+        gather_words(0)
+        gather_scales(0)
+        gather_words(1)
 
         nc.scalar.copy(out=w2_w[:].bitcast(U16).rearrange("p (t m) -> p m t", t=PACK), in_=w2_raw[:].bitcast(U16).rearrange("p (m t) -> p m t", t=PACK))
         nc.vector.tensor_copy(out=w2_s[:].rearrange("p (t m) -> p m t", t=PACK), in_=w2_sraw[:].rearrange("p (m t) -> p m t", t=PACK))
 
-        def cast_dealt(dst, raw, m0, m1):
+        def cast_dealt(dst, raw, m0, m1, engine="scalar"):
             out = dst[:].rearrange("p (t m j) -> p m j t", t=PACK, j=PACK)[:, m0:m1]
-            nc.scalar.copy(out=out, in_=raw.rearrange("p j (m t) -> p m j t", t=PACK))
+            src = raw.rearrange("p j (m t) -> p m j t", t=PACK)
+            if engine == "scalar":
+                nc.scalar.copy(out=out, in_=src)
+            elif engine == "vector":
+                nc.vector.tensor_copy(out=out, in_=src)
+            else:
+                nc.gpsimd.tensor_scalar(out=out, in0=src, scalar1=1.0, scalar2=0.0, op0=ALU.mult, op1=ALU.add)
+
+        def deal_wc():
+            for a in range(2):
+                nc.scalar.copy(
+                    out=wc_w[:, a * N : (a + 1) * N].rearrange("p (t m) -> p m t", t=PACK),
+                    in_=wc_raw[:, a * N : (a + 1) * N].bitcast(U32).rearrange("p (m t) -> p m t", t=PACK),
+                )
+
+        def deal_wc_scales():
+            nc.vector.tensor_copy(out=wc_s[:].rearrange("p (t m) -> p m t", t=PACK), in_=wc_sraw[:].rearrange("p (m t) -> p m t", t=PACK))
+
+        def cast_w1(i, engine="scalar"):
+            cast_dealt(w1_bf[i // 2], w1_raw[i][:], 64 * (i % 2), 64 * (i % 2 + 1), engine)
+
+        def cast_half(dst, raw, i, engine="scalar"):
+            cast_dealt(dst, raw[:, :, 256 * i : 256 * (i + 1)], 64 * i, 64 * (i + 1), engine)
 
         def quantised(name):
             return sb([P, 512], U32, name + "_w"), sb([P, 512], U8, name + "_s")
@@ -124,7 +154,7 @@ def tile_list_gust_front_page_kernel(
         h_bf = [[sb([P, PACK * HALF], BF16, "h_bf%d%d" % (g, h)) for h in range(2)] for g in range(2)]
         h_q = [[quantised("h_q%d%d" % (g, h)) for h in range(2)] for g in range(2)]
         tanh_sb = [sb([P, PACK * HALF], F32, "tanh%d" % h) for h in range(2)]
-        q_bf = [sb([P, PACK * HALF], BF16, "q_bf%d" % h) for h in range(2)]
+        q_bf = {}
         q_q = [quantised("q_q%d" % h) for h in range(2)]
         wc_w = sb([P, 2 * N], U32, "wc_w")
         wc_s = sb([P, N], U8, "wc_s")
@@ -151,19 +181,22 @@ def tile_list_gust_front_page_kernel(
         def spread(row):
             return row.unsqueeze(1).to_broadcast([P, CHUNK, PACK])
 
-        def make_tanh(h):
-            for c in range(HALF // CHUNK):
+        def make_tanh(h, chunks=range(HALF // CHUNK)):
+            for c in chunks:
                 acc = first_stage(lambda t: w2_w[:, 2 * P * t : 2 * P * (t + 1)].bitcast(FP4X4), w2_s, h, c)
                 nc.scalar.activation(out=woven(tanh_sb[h], c), in_=acc, func=ACT.Tanh)
 
-        def make_q(h):
-            nc.vector.tensor_tensor(
-                out=q_bf[h][:].rearrange("p (n t) -> p n t", t=PACK), in0=tanh_sb[h][:].rearrange("p (n t) -> p n t", t=PACK),
-                in1=qgain_sb[:].unsqueeze(1).to_broadcast([P, HALF, PACK]), op=ALU.mult,
-            )
+        def make_q(h, part, tag):
+            q_bf[h, part] = keep.tile([P, PACK * HALF // 2], BF16, name="q_bf%d%d" % (h, part), tag=tag, align_bytes=64)
+            for c in range(2):
+                nc.gpsimd.tensor_tensor(out=woven(q_bf[h, part], c), in0=woven(tanh_sb[h], 2 * part + c), in1=spread(qgain_sb[:]), op=ALU.mult)
 
-        def make_h(g, h):
-            for c in range(HALF // CHUNK):
+        def quantise_q(h, part):
+            cols = slice(part * HALF // 2, (part + 1) * HALF // 2)
+            nc.vector.quantize_mx(out=q_q[h][0][:, cols].bitcast(FP8X4), scales=q_q[h][1][:, cols], in_=q_bf[h, part][:])
+
+        def make_h(g, h, chunks=range(HALF // CHUNK)):
+            for c in chunks:
                 acc = first_stage(lambda t: w1_q[g][0][:, P * t : P * (t + 1)].bitcast(FP8X4), w1_q[g][1], h, c)
                 nc.vector.tensor_tensor(out=woven(h_bf[g][h], c), in0=acc, in1=spread(b1_sb[:, g, :]), op=ALU.add)
 
@@ -173,108 +206,104 @@ def tile_list_gust_front_page_kernel(
                 rhs=moving[0][:].bitcast(FP8X4), rhs_scale=moving[1][:], start=start, stop=stop,
             )
 
-        def make_d(h):
-            for t in range(PACK):
-                acc = bank()
-                for a in range(2):
-                    second_pass(acc, wc_w[:, a * N + t * P : a * N + (t + 1) * P], wc_s[4 * a :, t * P : (t + 1) * P], h_q[a][h], a == 0, a == 1)
-                nc.scalar.copy(out=d_sb[t][:, h * HALF : (h + 1) * HALF], in_=acc[:])
+        def make_d(t, h):
+            acc = bank()
+            for a in range(2):
+                second_pass(acc, wc_w[:, a * N + t * P : a * N + (t + 1) * P], wc_s[4 * a :, t * P : (t + 1) * P], h_q[a][h], a == 0, a == 1)
+            nc.scalar.copy(out=d_sb[t][:, h * HALF : (h + 1) * HALF], in_=acc[:])
 
-        def open_e(h):
-            accs = [bank() for t in range(PACK)]
-            for t in range(PACK):
-                cols = slice(t * P, (t + 1) * P)
-                for a in range(2):
-                    second_pass(accs[t], wa_q[a][0][:, cols], wa_q[a][1][:, cols], h_q[a][h], a == 0, False)
-            return accs
-
-        def close_e(accs, h):
-            for t in range(PACK):
-                cols = slice(t * P, (t + 1) * P)
-                second_pass(accs[t], wb_q[0][:, cols], wb_q[1][:, cols], q_q[h], False, True)
-
-        def empty_e(accs, h, t):
+        def make_e(t, h):
+            acc = bank()
+            cols = slice(t * P, (t + 1) * P)
             col = slice(t, t + 1)
+            for a in range(2):
+                second_pass(acc, wa_q[a][0][:, cols], wa_q[a][1][:, cols], h_q[a][h], a == 0, False)
+            second_pass(acc, wb_q[0][:, cols], wb_q[1][:, cols], q_q[h], False, True)
             nc.vector.tensor_scalar(
-                out=e_sb[t][:, h * HALF : (h + 1) * HALF], in0=accs[t][:], scalar1=1.0,
+                out=e_sb[t][:, h * HALF : (h + 1) * HALF], in0=acc[:], scalar1=1.0,
                 scalar2=(None if h == 0 else top0[:, col]), op0=ALU.mult, op1=ALU.max,
                 accum_out=(top0 if h == 0 else top)[:, col],
             )
 
-        cast_dealt(w1_bf[0], w1_raw[0][:], 0, 64)
-        cast_dealt(w1_bf[0], w1_raw[1][:], 64, 128)
+        cast_w1(0)
+        cast_w1(1)
         quantise(w1_q[0], w1_bf[0])
-        make_h(0, 0)
-        make_tanh(0)
-        cast_dealt(w1_bf[1], w1_raw[2][:], 0, 64)
-        cast_dealt(w1_bf[1], w1_raw[3][:], 64, 128)
-        make_q(0)
-        quantise(h_q[0][0], h_bf[0][0])
+        gather_scales(1)
+        deal_wc()
+        make_tanh(0, [0, 1])
+        make_h(0, 0, [0])
+        make_tanh(0, [2])
+        make_h(0, 0, [1])
+        make_tanh(0, [3])
+        make_h(0, 0, [2, 3])
+        make_q(0, 0, "q_bf_a")
+        make_q(0, 1, "q_bf_b")
+        make_h(0, 1)
+        cast_w1(2)
+        cast_w1(3)
+        make_tanh(1)
         quantise(w1_q[1], w1_bf[1])
-        quantise(q_q[0], q_bf[0])
+        quantise(h_q[0][0], h_bf[0][0])
+        quantise_q(0, 0)
+        quantise_q(0, 1)
+        make_q(1, 0, "q_bf_b")
         make_h(1, 0)
-        for a in range(2):
-            nc.scalar.copy(
-                out=wc_w[:, a * N : (a + 1) * N].rearrange("p (t m) -> p m t", t=PACK),
-                in_=wc_raw[:, a * N : (a + 1) * N].bitcast(U32).rearrange("p (m t) -> p m t", t=PACK),
-            )
-        nc.vector.tensor_copy(out=wc_s[:].rearrange("p (t m) -> p m t", t=PACK), in_=wc_sraw[:].rearrange("p (m t) -> p m t", t=PACK))
         quantise(h_q[1][0], h_bf[1][0])
+        deal_wc_scales()
+        quantise(h_q[0][1], h_bf[0][1])
+        make_q(1, 1, "h_bf01")
         for a in range(2):
             for i in range(2):
-                cast_dealt(wa_bf[a], wa_raw[a][:, :, 256 * i : 256 * (i + 1)], 64 * i, 64 * (i + 1))
-        make_h(0, 1)
-        quantise(wa_q[0], wa_bf[0])
-        quantise(h_q[0][1], h_bf[0][1])
+                cast_half(wa_bf[a], wa_raw[a], i)
         for i in range(2):
-            cast_dealt(wb_bf, wb_raw[:, :, 256 * i : 256 * (i + 1)], 64 * i, 64 * (i + 1))
-        make_tanh(1)
+            cast_half(wb_bf, wb_raw, i)
         make_h(1, 1)
-        quantise(wa_q[1], wa_bf[1])
-        quantise(h_q[1][1], h_bf[1][1])
-        quantise(wb_q, wb_bf)
-        make_d(0)
-        e0 = open_e(0)
-        close_e(e0, 0)
-        make_q(1)
-        nc.vector.scalar_tensor_tensor(out=slope[:], in0=steep_sb[:], scalar=-1.0, in1=share_sb[:], op0=ALU.mult, op1=ALU.mult)
-        quantise(q_q[1], q_bf[1])
-        make_d(1)
         for t in range(PACK):
-            empty_e(e0, 0, t)
-        e1 = open_e(1)
-        close_e(e1, 1)
+            make_d(t, 0)
+        quantise(h_q[1][1], h_bf[1][1])
+        quantise(wa_q[0], wa_bf[0])
+        quantise(wa_q[1], wa_bf[1])
+        quantise(wb_q, wb_bf)
+        quantise_q(1, 0)
+        quantise_q(1, 1)
+        nc.vector.scalar_tensor_tensor(out=slope[:], in0=steep_sb[:], scalar=-1.0, in1=share_sb[:], op0=ALU.mult, op1=ALU.mult)
 
         PART = PICKS // 2
-        gate = [sb([P, PACK, PART], F32, "gate%d" % c) for c in range(2)]
-        summed = [sb([P, PACK, PART], F32, "summed%d" % c) for c in range(2)]
-        y = [sb([P, PACK, PART], F32, "y%d" % c) for c in range(2)]
+        gate = sb([P, PACK, PICKS], F32, "gate")
+        summed = sb([P, PACK, PICKS], F32, "summed")
+        y = sb([P, PACK, PICKS], F32, "y")
         y_bf = [sb([P, PACK * PART], BF16, "y_bf%d" % c) for c in range(2)]
         y_w = [sb([P, PART], U32, "y_w%d" % c) for c in range(2)]
         y_s = sb([P, PICKS], U8, "y_s")
         out_rows = out_0.rearrange("(p t) c -> p t c", t=PACK)
         out_words = out_1[0].rearrange("p m t -> p (m t)").bitcast(I32)
 
-        def look(t, c):
+        def scores(t):
             col = slice(t, t + 1)
-            picks = pos1_sb[:, c * PART // 16 : (c + 1) * PART // 16]
-            nc.scalar.activation(out=gate[c][:, t, :], in_=e_sb[t][:].indirect(picks), func=ACT.Sigmoid, bias=bias[:, col], scale=steep_sb[:, col])
+            make_e(t, 0)
+            make_e(t, 1)
+            nc.vector.tensor_tensor(out=bias[:, col], in0=top[:, col], in1=slope[:, col], op=ALU.mult)
 
-        def combine(pair, c):
-            rows = slice(2 * pair, 2 * pair + 2)
-            cols = slice(c * PART, (c + 1) * PART)
-            picks = pos2_sb[:, c * PART // 16 : (c + 1) * PART // 16]
-            nc.vector.tensor_tensor(out=gate[c][:, rows, :], in0=gate[c][:, rows, :], in1=mat_sb[:, rows, cols], op=ALU.mult)
-            for t in range(2 * pair, 2 * pair + 2):
-                nc.vector.tensor_tensor(out=summed[c][:, t, :], in0=d_sb[t][:].indirect(picks), in1=gate[c][:, t, :], op=ALU.add)
-            for t in range(2 * pair, 2 * pair + 2):
-                nc.scalar.activation(out=y[c][:, t, :], in_=summed[c][:, t, :], func=ACT.Copy, scale=gain_sb[:, t : t + 1])
-            nc.sync.dma_start(out=out_rows[:, rows, cols], in_=y[c][:, rows, :])
+        def look(t, c0, c1):
+            col = slice(t, t + 1)
+            nc.scalar.activation(
+                out=gate[:, t, c0:c1], in_=e_sb[t][:].indirect(pos1_sb[:, c0 // 16 : c1 // 16]),
+                func=ACT.Sigmoid, bias=bias[:, col], scale=steep_sb[:, col],
+            )
+
+        def combine(t, c0, c1, last=False):
+            nc.vector.tensor_tensor(out=gate[:, t, c0:c1], in0=gate[:, t, c0:c1], in1=mat_sb[:, t, c0:c1], op=ALU.mult)
+            nc.vector.tensor_tensor(out=summed[:, t, c0:c1], in0=d_sb[t][:].indirect(pos2_sb[:, c0 // 16 : c1 // 16]), in1=gate[:, t, c0:c1], op=ALU.add)
+            if last:
+                nc.vector.tensor_scalar(out=y[:, t, c0:c1], in0=summed[:, t, c0:c1], scalar1=gain_sb[:, t : t + 1], scalar2=None, op0=ALU.mult)
+            else:
+                nc.scalar.activation(out=y[:, t, c0:c1], in_=summed[:, t, c0:c1], func=ACT.Copy, scale=gain_sb[:, t : t + 1])
+            nc.sync.dma_start(out=out_rows[:, t, c0:c1], in_=y[:, t, c0:c1])
 
         def planes(c, split):
             cols = slice(c * PART, (c + 1) * PART)
             woven_y = y_bf[c][:].rearrange("p (c i t) -> p c t i", i=4, t=PACK)
-            rows_y = y[c][:].rearrange("p t (c i) -> p c t i", i=4)
+            rows_y = y[:, :, cols].rearrange("p t (c i) -> p c t i", i=4)
             if split:
                 nc.vector.tensor_copy(out=woven_y[:, :split], in_=rows_y[:, :split])
             nc.scalar.copy(out=woven_y[:, split:], in_=rows_y[:, split:])
@@ -282,17 +311,18 @@ def tile_list_gust_front_page_kernel(
             nc.sync.dma_start(out=out_words[:, cols], in_=y_w[c][:].bitcast(I32))
 
         for t in range(PACK):
-            col = slice(t, t + 1)
-            empty_e(e1, 1, t)
-            nc.vector.tensor_tensor(out=bias[:, col], in0=top[:, col], in1=slope[:, col], op=ALU.mult)
-            look(t, 0)
-        for t in range(PACK):
-            look(t, 1)
-        combine(0, 0)
-        combine(1, 0)
-        combine(0, 1)
+            scores(t)
+            look(t, 0, PICKS if t < 2 else PART)
+            make_d(t, 1)
+        look(2, PART, PICKS)
+        look(3, PART, PICKS)
+        combine(0, 0, PICKS)
+        combine(1, 0, PICKS)
+        combine(2, 0, PART)
+        combine(3, 0, PART)
         planes(0, 0)
-        combine(1, 1)
+        combine(2, PART, PICKS)
+        combine(3, PART, PICKS, last=True)
         planes(1, 42)
         for q in range(QUADS):
             queue = nc.scalar if q % 2 else nc.sync

@@ -67,51 +67,51 @@ def tile_list_gust_front_page_kernel(
             nc.sync.dma_start(out=vec_sb[:], in_=vec.rearrange("(p t) -> p t", t=PACK))
 
         w1_rows = w1.rearrange("(p j) c -> p j c", j=PACK)
-        nc.sync.dma_start(out=tab_w[:], in_=tab_words[0].rearrange("p t i -> p (t i)").bitcast(I32))
         nc.sync.dma_start(offs_sb[:], offs)
+        nc.sync.dma_start(pos1_sb[:], pos1)
+        nc.sync.dma_start(pos2_sb[:], pos2)
         for q in range(QUADS):
             nc.sync.dma_start(out=tab_s[32 * q : 32 * q + 4, :].bitcast(I32), in_=tab_scales[0, 4 * q : 4 * q + 4, :].bitcast(I32))
-        for i in range(2):
-            nc.sync.dma_start(out=w1_raw[i][:], in_=w1_rows[:, :, 256 * i : 256 * (i + 1)])
+        nc.sync.dma_start(out=tab_w[:], in_=tab_words[0].rearrange("p t i -> p (t i)").bitcast(I32))
         nc.sync.dma_start(out=w2_raw[:].bitcast(I32), in_=w2_words[0].bitcast(I32))
         for q in range(QUADS):
             nc.sync.dma_start(out=w2_sraw[32 * q : 32 * q + 4, :].bitcast(I32), in_=w2_scales[0, 4 * q : 4 * q + 4, :].bitcast(I32))
-        nc.sync.dma_start(out=wc_raw[:].rearrange("p (a c) -> p a c", a=2), in_=wc_words.rearrange("a p c i -> p a (c i)").bitcast(I32))
+        for i in range(2):
+            nc.sync.dma_start(out=w1_raw[i][:], in_=w1_rows[:, :, 256 * i : 256 * (i + 1)])
         nc.sync.dma_start(out=w1_raw[2][:], in_=w1_rows[:, :, 512:768])
         nc.sync.dma_start(out=b1_sb[:], in_=b1.rearrange("(g p t) -> p g t", g=2, t=PACK))
         load_vector(qgain_sb, qgain)
         nc.sync.dma_start(out=w1_raw[3][:], in_=w1_rows[:, :, 768:1024])
+        nc.sync.dma_start(out=wc_raw[:].rearrange("p (a c) -> p a c", a=2), in_=wc_words.rearrange("a p c i -> p a (c i)").bitcast(I32))
         for a in range(2):
             nc.sync.dma_start(out=wa_raw[a][:], in_=wa[GROUP * a : GROUP * (a + 1), :].rearrange("(p j) c -> p j c", j=PACK))
         for q in range(QUADS):
             nc.sync.dma_start(out=wc_sraw[32 * q : 32 * q + 8, :].bitcast(I32), in_=wc_scales[:, 4 * q : 4 * q + 4, :].bitcast(I32))
         nc.sync.dma_start(out=wb_raw[:], in_=wb.rearrange("(p j) c -> p j c", j=PACK))
         nc.sync.dma_start(out=mat_sb[:], in_=mat.rearrange("(p t) c -> p t c", t=PACK))
-        nc.sync.dma_start(pos1_sb[:], pos1)
-        nc.sync.dma_start(pos2_sb[:], pos2)
         for vec_sb, vec in ((steep_sb, steep), (share_sb, share), (gain_sb, gain)):
             load_vector(vec_sb, vec)
 
         w2_w = sb([P, 2 * M], U8, "w2_w")
-        w2_s = sb([P, M], U8, "w2_s")
 
-        v_w = [sb([P, HALF], U32, "v_w%d" % h) for h in range(2)]
-        v_s = [sb([P, HALF], U8, "v_s0")]
+        v_w = [sb([P, HALF], U32, "v_w0")]
+        v_s = [sb([P, HALF], U8, "v_s%d" % h) for h in range(2)]
 
         def gather_words(h):
             nc.vector.tensor_copy(v_w[h][:], tab_w[:].bitcast(U32).indirect(offs_sb[:, h * HALF // 16 : (h + 1) * HALF // 16]))
 
         def gather_scales(h):
-            if h:
-                v_s.append(keep.tile([P, HALF], U8, name="v_s1", tag="w1_bf0", align_bytes=64))
             nc.vector.tensor_copy(v_s[h][:], tab_s[:].indirect(offs_sb[:, h * HALF // 16 : (h + 1) * HALF // 16]))
 
-        gather_words(0)
         gather_scales(0)
+        gather_scales(1)
+        gather_words(0)
+        w2_s = sb([P, M], U8, "w2_s")
+        nc.vector.tensor_copy(out=w2_s[:].rearrange("p (t m) -> p m t", t=PACK), in_=w2_sraw[:].rearrange("p (m t) -> p m t", t=PACK))
+        v_w.append(keep.tile([P, HALF], U32, name="v_w1", tag="w2_sraw", align_bytes=64))
         gather_words(1)
 
         nc.scalar.copy(out=w2_w[:].bitcast(U16).rearrange("p (t m) -> p m t", t=PACK), in_=w2_raw[:].bitcast(U16).rearrange("p (m t) -> p m t", t=PACK))
-        nc.vector.tensor_copy(out=w2_s[:].rearrange("p (t m) -> p m t", t=PACK), in_=w2_sraw[:].rearrange("p (m t) -> p m t", t=PACK))
 
         def cast_dealt(dst, raw, m0, m1, engine="scalar"):
             out = dst[:].rearrange("p (t m j) -> p m j t", t=PACK, j=PACK)[:, m0:m1]
@@ -123,9 +123,9 @@ def tile_list_gust_front_page_kernel(
             else:
                 nc.gpsimd.tensor_scalar(out=out, in0=src, scalar1=1.0, scalar2=0.0, op0=ALU.mult, op1=ALU.add)
 
-        def deal_wc():
+        def deal_wc(copy):
             for a in range(2):
-                nc.scalar.copy(
+                copy(
                     out=wc_w[:, a * N : (a + 1) * N].rearrange("p (t m) -> p m t", t=PACK),
                     in_=wc_raw[:, a * N : (a + 1) * N].bitcast(U32).rearrange("p (m t) -> p m t", t=PACK),
                 )
@@ -186,14 +186,16 @@ def tile_list_gust_front_page_kernel(
                 acc = first_stage(lambda t: w2_w[:, 2 * P * t : 2 * P * (t + 1)].bitcast(FP4X4), w2_s, h, c)
                 nc.scalar.activation(out=woven(tanh_sb[h], c), in_=acc, func=ACT.Tanh)
 
-        def make_q(h, part, tag):
-            q_bf[h, part] = keep.tile([P, PACK * HALF // 2], BF16, name="q_bf%d%d" % (h, part), tag=tag, align_bytes=64)
-            for c in range(2):
-                nc.gpsimd.tensor_tensor(out=woven(q_bf[h, part], c), in0=woven(tanh_sb[h], 2 * part + c), in1=spread(qgain_sb[:]), op=ALU.mult)
+        def make_q(h, chunks, engine, tag):
+            tile = keep.tile([P, len(chunks) * GROUP], BF16, name="q_bf%d%d" % (h, chunks[0]), tag=tag, align_bytes=64)
+            q_bf[h, chunks[0]] = tile, len(chunks)
+            for i, c in enumerate(chunks):
+                engine.tensor_tensor(out=woven(tile, i), in0=woven(tanh_sb[h], c), in1=spread(qgain_sb[:]), op=ALU.mult)
 
-        def quantise_q(h, part):
-            cols = slice(part * HALF // 2, (part + 1) * HALF // 2)
-            nc.vector.quantize_mx(out=q_q[h][0][:, cols].bitcast(FP8X4), scales=q_q[h][1][:, cols], in_=q_bf[h, part][:])
+        def quantise_q(h, c):
+            tile, count = q_bf[h, c]
+            cols = slice(c * CHUNK, (c + count) * CHUNK)
+            nc.vector.quantize_mx(out=q_q[h][0][:, cols].bitcast(FP8X4), scales=q_q[h][1][:, cols], in_=tile[:])
 
         def make_h(g, h, chunks=range(HALF // CHUNK)):
             for c in chunks:
@@ -226,46 +228,43 @@ def tile_list_gust_front_page_kernel(
             )
 
         cast_w1(0)
-        cast_w1(1)
+        make_tanh(0)
+        cast_w1(1, "vector")
         quantise(w1_q[0], w1_bf[0])
-        gather_scales(1)
-        deal_wc()
-        make_tanh(0, [0, 1])
-        make_h(0, 0, [0])
-        make_tanh(0, [2])
-        make_h(0, 0, [1])
-        make_tanh(0, [3])
-        make_h(0, 0, [2, 3])
-        make_q(0, 0, "q_bf_a")
-        make_q(0, 1, "q_bf_b")
+        make_q(0, [0, 1, 2], nc.gpsimd, "w1_bf0")
+        make_h(0, 0)
         make_h(0, 1)
         cast_w1(2)
         cast_w1(3)
         make_tanh(1)
+        deal_wc(nc.scalar.copy)
         quantise(w1_q[1], w1_bf[1])
         quantise(h_q[0][0], h_bf[0][0])
-        quantise_q(0, 0)
-        quantise_q(0, 1)
-        make_q(1, 0, "q_bf_b")
-        make_h(1, 0)
-        quantise(h_q[1][0], h_bf[1][0])
         deal_wc_scales()
         quantise(h_q[0][1], h_bf[0][1])
-        make_q(1, 1, "h_bf01")
-        for a in range(2):
-            for i in range(2):
-                cast_half(wa_bf[a], wa_raw[a], i)
-        for i in range(2):
-            cast_half(wb_bf, wb_raw, i)
+        make_q(1, [0, 1, 2], nc.gpsimd, "h_bf01")
+        make_h(1, 0)
         make_h(1, 1)
-        for t in range(PACK):
-            make_d(t, 0)
+        cast_half(wa_bf[0], wa_raw[0], 0)
+        cast_half(wa_bf[0], wa_raw[0], 1)
+        cast_half(wa_bf[1], wa_raw[1], 0)
+        cast_half(wa_bf[1], wa_raw[1], 1)
+        quantise(h_q[1][0], h_bf[1][0])
         quantise(h_q[1][1], h_bf[1][1])
+        for h in range(2):
+            for t in range(PACK):
+                make_d(t, h)
         quantise(wa_q[0], wa_bf[0])
+        cast_half(wb_bf, wb_raw, 0, "vector")
+        cast_half(wb_bf, wb_raw, 1, "vector")
         quantise(wa_q[1], wa_bf[1])
+        make_q(0, [3], nc.vector, "qc")
         quantise(wb_q, wb_bf)
+        quantise_q(0, 0)
+        quantise_q(0, 3)
+        make_q(1, [3], nc.vector, "qd")
         quantise_q(1, 0)
-        quantise_q(1, 1)
+        quantise_q(1, 3)
         nc.vector.scalar_tensor_tensor(out=slope[:], in0=steep_sb[:], scalar=-1.0, in1=share_sb[:], op0=ALU.mult, op1=ALU.mult)
 
         PART = PICKS // 2
@@ -282,7 +281,7 @@ def tile_list_gust_front_page_kernel(
             col = slice(t, t + 1)
             make_e(t, 0)
             make_e(t, 1)
-            nc.vector.tensor_tensor(out=bias[:, col], in0=top[:, col], in1=slope[:, col], op=ALU.mult)
+            nc.scalar.activation(out=bias[:, col], in_=top[:, col], func=ACT.Copy, scale=slope[:, col])
 
         def look(t, c0, c1):
             col = slice(t, t + 1)
@@ -313,7 +312,6 @@ def tile_list_gust_front_page_kernel(
         for t in range(PACK):
             scores(t)
             look(t, 0, PICKS if t < 2 else PART)
-            make_d(t, 1)
         look(2, PART, PICKS)
         look(3, PART, PICKS)
         combine(0, 0, PICKS)

@@ -74,23 +74,24 @@ def tile_list_gust_front_page_kernel(
             nc.sync.dma_start(out=tab_s[32 * q : 32 * q + 4, :].bitcast(I32), in_=tab_scales[0, 4 * q : 4 * q + 4, :].bitcast(I32))
         nc.sync.dma_start(out=tab_w[:], in_=tab_words[0].rearrange("p t i -> p (t i)").bitcast(I32))
         nc.sync.dma_start(out=w2_raw[:].bitcast(I32), in_=w2_words[0].bitcast(I32))
+        nc.sync.dma_start(out=w1_raw[0][:], in_=w1_rows[:, :, 0:256])
         for q in range(QUADS):
             nc.sync.dma_start(out=w2_sraw[32 * q : 32 * q + 4, :].bitcast(I32), in_=w2_scales[0, 4 * q : 4 * q + 4, :].bitcast(I32))
-        for i in range(2):
-            nc.sync.dma_start(out=w1_raw[i][:], in_=w1_rows[:, :, 256 * i : 256 * (i + 1)])
+        nc.sync.dma_start(out=w1_raw[1][:], in_=w1_rows[:, :, 256:512])
         nc.sync.dma_start(out=w1_raw[2][:], in_=w1_rows[:, :, 512:768])
         nc.sync.dma_start(out=b1_sb[:], in_=b1.rearrange("(g p t) -> p g t", g=2, t=PACK))
         load_vector(qgain_sb, qgain)
         nc.sync.dma_start(out=w1_raw[3][:], in_=w1_rows[:, :, 768:1024])
         nc.sync.dma_start(out=wc_raw[:].rearrange("p (a c) -> p a c", a=2), in_=wc_words.rearrange("a p c i -> p a (c i)").bitcast(I32))
-        for a in range(2):
-            nc.sync.dma_start(out=wa_raw[a][:], in_=wa[GROUP * a : GROUP * (a + 1), :].rearrange("(p j) c -> p j c", j=PACK))
         for q in range(QUADS):
             nc.sync.dma_start(out=wc_sraw[32 * q : 32 * q + 8, :].bitcast(I32), in_=wc_scales[:, 4 * q : 4 * q + 4, :].bitcast(I32))
+        nc.sync.dma_start(out=wa_raw[0][:], in_=wa[0:GROUP, :].rearrange("(p j) c -> p j c", j=PACK))
+        nc.sync.dma_start(out=wa_raw[1][:], in_=wa[GROUP : 2 * GROUP, :].rearrange("(p j) c -> p j c", j=PACK))
         nc.sync.dma_start(out=wb_raw[:], in_=wb.rearrange("(p j) c -> p j c", j=PACK))
+        load_vector(steep_sb, steep)
+        load_vector(share_sb, share)
         nc.sync.dma_start(out=mat_sb[:], in_=mat.rearrange("(p t) c -> p t c", t=PACK))
-        for vec_sb, vec in ((steep_sb, steep), (share_sb, share), (gain_sb, gain)):
-            load_vector(vec_sb, vec)
+        load_vector(gain_sb, gain)
 
         w2_w = sb([P, 2 * M], U8, "w2_w")
 
@@ -151,7 +152,7 @@ def tile_list_gust_front_page_kernel(
         w1_q = [quantised("w1_q%d" % g) for g in range(2)]
         wa_q = [quantised("wa_q%d" % a) for a in range(2)]
         wb_q = quantised("wb_q")
-        h_bf = [[sb([P, PACK * HALF], BF16, "h_bf%d%d" % (g, h)) for h in range(2)] for g in range(2)]
+        h_bf = [[sb([P, PACK * HALF], BF16, "h_bf0%d" % h) for h in range(2)], []]
         h_q = [[quantised("h_q%d%d" % (g, h)) for h in range(2)] for g in range(2)]
         tanh_sb = [sb([P, PACK * HALF], F32, "tanh%d" % h) for h in range(2)]
         q_bf = {}
@@ -228,8 +229,9 @@ def tile_list_gust_front_page_kernel(
             )
 
         cast_w1(0)
+        cast_dealt(w1_bf[0], w1_raw[1][:, :, :128], 64, 96)
+        cast_dealt(w1_bf[0], w1_raw[1][:, :, 128:], 96, 128, "vector")
         make_tanh(0)
-        cast_w1(1, "vector")
         quantise(w1_q[0], w1_bf[0])
         make_q(0, [0, 1, 2], nc.gpsimd, "w1_bf0")
         make_h(0, 0)
@@ -239,30 +241,31 @@ def tile_list_gust_front_page_kernel(
         make_tanh(1)
         deal_wc(nc.scalar.copy)
         quantise(w1_q[1], w1_bf[1])
-        quantise(h_q[0][0], h_bf[0][0])
         deal_wc_scales()
+        quantise(h_q[0][0], h_bf[0][0])
         quantise(h_q[0][1], h_bf[0][1])
         make_q(1, [0, 1, 2], nc.gpsimd, "h_bf01")
+        h_bf[1].append(keep.tile([P, PACK * HALF], BF16, name="h_bf10", tag="wc_sraw", align_bytes=64))
+        h_bf[1].append(sb([P, PACK * HALF], BF16, "h_bf11"))
         make_h(1, 0)
         make_h(1, 1)
-        cast_half(wa_bf[0], wa_raw[0], 0)
-        cast_half(wa_bf[0], wa_raw[0], 1)
-        cast_half(wa_bf[1], wa_raw[1], 0)
-        cast_half(wa_bf[1], wa_raw[1], 1)
+        for a in range(2):
+            for i in range(2):
+                cast_half(wa_bf[a], wa_raw[a], i)
+        for i in range(2):
+            cast_half(wb_bf, wb_raw, i)
         quantise(h_q[1][0], h_bf[1][0])
         quantise(h_q[1][1], h_bf[1][1])
         for h in range(2):
             for t in range(PACK):
                 make_d(t, h)
         quantise(wa_q[0], wa_bf[0])
-        cast_half(wb_bf, wb_raw, 0, "vector")
-        cast_half(wb_bf, wb_raw, 1, "vector")
-        quantise(wa_q[1], wa_bf[1])
         make_q(0, [3], nc.vector, "qc")
-        quantise(wb_q, wb_bf)
+        quantise(wa_q[1], wa_bf[1])
+        make_q(1, [3], nc.vector, "qd")
         quantise_q(0, 0)
         quantise_q(0, 3)
-        make_q(1, [3], nc.vector, "qd")
+        quantise(wb_q, wb_bf)
         quantise_q(1, 0)
         quantise_q(1, 3)
         nc.vector.scalar_tensor_tensor(out=slope[:], in0=steep_sb[:], scalar=-1.0, in1=share_sb[:], op0=ALU.mult, op1=ALU.mult)
@@ -281,7 +284,7 @@ def tile_list_gust_front_page_kernel(
             col = slice(t, t + 1)
             make_e(t, 0)
             make_e(t, 1)
-            nc.scalar.activation(out=bias[:, col], in_=top[:, col], func=ACT.Copy, scale=slope[:, col])
+            nc.vector.tensor_tensor(out=bias[:, col], in0=top[:, col], in1=slope[:, col], op=ALU.mult)
 
         def look(t, c0, c1):
             col = slice(t, t + 1)
@@ -321,7 +324,7 @@ def tile_list_gust_front_page_kernel(
         planes(0, 0)
         combine(2, PART, PICKS)
         combine(3, PART, PICKS, last=True)
-        planes(1, 42)
+        planes(1, 36)
         for q in range(QUADS):
             queue = nc.scalar if q % 2 else nc.sync
             queue.dma_start(out=out_2[0, 4 * q : 4 * q + 4, :].bitcast(I32), in_=y_s[32 * q : 32 * q + 4, :].bitcast(I32))

@@ -19,9 +19,18 @@ ALU = mybir.AluOpType
 P = 128
 PACK = 4
 GROUP = P * PACK
-HALF = 512
-CHUNK = 128
+BANK = 512
+BANKS = 8
+HALF = S // 2
+CHUNK = BANK // PACK
+CHUNKS = HALF // CHUNK
+PIECE = 256
 QUADS = 4
+LIST = 16
+PART = PICKS // 2
+GPSIMD_CHUNKS = [0, 1, 2]
+VECTOR_CHUNKS = [3]
+VECTOR_RUNS = 36
 
 
 def tile_list_gust_front_page_kernel(
@@ -31,17 +40,17 @@ def tile_list_gust_front_page_kernel(
     nc = tc.nc
     with ExitStack() as ctx:
         keep = ctx.enter_context(tc.tile_pool(name="keep", bufs=1))
-        psum = ctx.enter_context(tc.psum_pool(name="psum", bufs=8))
+        psum = ctx.enter_context(tc.psum_pool(name="psum", bufs=BANKS))
 
-        def sb(shape, dtype, name):
-            return keep.tile(shape, dtype, name=name, align_bytes=64)
+        def sb(shape, dtype, name, tag=None):
+            return keep.tile(shape, dtype, name=name, tag=tag or name, align_bytes=64)
 
         def bank():
-            return psum.tile([P, 512], F32, name="bank")
+            return psum.tile([P, BANK], F32, name="bank")
 
-        offs_sb = keep.tile([P, S // 16], U16, name="offs_sb")
-        pos1_sb = keep.tile([P, PICKS // 16], U16, name="pos1_sb")
-        pos2_sb = keep.tile([P, PICKS // 16], U16, name="pos2_sb")
+        offs_sb = keep.tile([P, S // LIST], U16, name="offs_sb")
+        pos1_sb = keep.tile([P, PICKS // LIST], U16, name="pos1_sb")
+        pos2_sb = keep.tile([P, PICKS // LIST], U16, name="pos2_sb")
 
         tab_w = sb([P, T], I32, "tab_w")
         tab_s = sb([P, T], U8, "tab_s")
@@ -49,7 +58,7 @@ def tile_list_gust_front_page_kernel(
         w2_sraw = sb([P, M], U8, "w2_sraw")
         wc_raw = sb([P, 2 * N], I32, "wc_raw")
         wc_sraw = sb([P, N], U8, "wc_sraw")
-        w1_raw = [sb([P, PACK, 256], F32, "w1_raw%d" % i) for i in range(4)]
+        w1_raw = [sb([P, PACK, PIECE], F32, "w1_raw%d" % i) for i in range(H // PIECE)]
         wa_raw = [sb([P, PACK, N], F32, "wa_raw%d" % a) for a in range(2)]
         wb_raw = sb([P, PACK, N], F32, "wb_raw")
         mat_sb = sb([P, PACK, PICKS], F32, "mat_sb")
@@ -66,85 +75,69 @@ def tile_list_gust_front_page_kernel(
         def load_vector(vec_sb, vec):
             nc.sync.dma_start(out=vec_sb[:], in_=vec.rearrange("(p t) -> p t", t=PACK))
 
-        w1_rows = w1.rearrange("(p j) c -> p j c", j=PACK)
+        def load_rows(raw, rows):
+            nc.sync.dma_start(out=raw[:], in_=rows.rearrange("(p j) c -> p j c", j=PACK))
+
+        def load_scales(tile, rows_of):
+            for q in range(QUADS):
+                rows = rows_of(slice(4 * q, 4 * q + 4))
+                count = 4 * (rows.shape[0] if rows.ndim == 3 else 1)
+                nc.sync.dma_start(out=tile[32 * q : 32 * q + count, :].bitcast(I32), in_=rows.bitcast(I32))
+
+        def load_w1(i):
+            load_rows(w1_raw[i], w1[:, PIECE * i : PIECE * (i + 1)])
+
         nc.sync.dma_start(offs_sb[:], offs)
         nc.sync.dma_start(pos1_sb[:], pos1)
         nc.sync.dma_start(pos2_sb[:], pos2)
-        for q in range(QUADS):
-            nc.sync.dma_start(out=tab_s[32 * q : 32 * q + 4, :].bitcast(I32), in_=tab_scales[0, 4 * q : 4 * q + 4, :].bitcast(I32))
+        load_scales(tab_s, lambda rows: tab_scales[0, rows, :])
         nc.sync.dma_start(out=tab_w[:], in_=tab_words[0].rearrange("p t i -> p (t i)").bitcast(I32))
         nc.sync.dma_start(out=w2_raw[:].bitcast(I32), in_=w2_words[0].bitcast(I32))
-        nc.sync.dma_start(out=w1_raw[0][:], in_=w1_rows[:, :, 0:256])
-        for q in range(QUADS):
-            nc.sync.dma_start(out=w2_sraw[32 * q : 32 * q + 4, :].bitcast(I32), in_=w2_scales[0, 4 * q : 4 * q + 4, :].bitcast(I32))
-        nc.sync.dma_start(out=w1_raw[1][:], in_=w1_rows[:, :, 256:512])
-        nc.sync.dma_start(out=w1_raw[2][:], in_=w1_rows[:, :, 512:768])
+        load_w1(0)
+        load_scales(w2_sraw, lambda rows: w2_scales[0, rows, :])
+        load_w1(1)
+        load_w1(2)
         nc.sync.dma_start(out=b1_sb[:], in_=b1.rearrange("(g p t) -> p g t", g=2, t=PACK))
         load_vector(qgain_sb, qgain)
-        nc.sync.dma_start(out=w1_raw[3][:], in_=w1_rows[:, :, 768:1024])
-        nc.sync.dma_start(out=wc_raw[:].rearrange("p (a c) -> p a c", a=2), in_=wc_words.rearrange("a p c i -> p a (c i)").bitcast(I32))
-        for q in range(QUADS):
-            nc.sync.dma_start(out=wc_sraw[32 * q : 32 * q + 8, :].bitcast(I32), in_=wc_scales[:, 4 * q : 4 * q + 4, :].bitcast(I32))
-        nc.sync.dma_start(out=wa_raw[0][:], in_=wa[0:GROUP, :].rearrange("(p j) c -> p j c", j=PACK))
-        nc.sync.dma_start(out=wa_raw[1][:], in_=wa[GROUP : 2 * GROUP, :].rearrange("(p j) c -> p j c", j=PACK))
-        nc.sync.dma_start(out=wb_raw[:], in_=wb.rearrange("(p j) c -> p j c", j=PACK))
+        load_w1(3)
+        nc.sync.dma_start(
+            out=wc_raw[:].rearrange("p (a c) -> p a c", a=2),
+            in_=wc_words.rearrange("a p c i -> p a (c i)").bitcast(I32),
+        )
+        load_scales(wc_sraw, lambda rows: wc_scales[:, rows, :])
+        for a in range(2):
+            load_rows(wa_raw[a], wa[GROUP * a : GROUP * (a + 1), :])
+        load_rows(wb_raw, wb)
         load_vector(steep_sb, steep)
         load_vector(share_sb, share)
-        nc.sync.dma_start(out=mat_sb[:], in_=mat.rearrange("(p t) c -> p t c", t=PACK))
+        load_rows(mat_sb, mat)
         load_vector(gain_sb, gain)
 
-        w2_w = sb([P, 2 * M], U8, "w2_w")
+        def picks(list_sb, j0, j1):
+            return list_sb[:, j0 // LIST : j1 // LIST]
 
+        def deal(copy, dst, src):
+            copy(out=dst.rearrange("p (t m) -> p t m", t=PACK), in_=src.rearrange("p (m t) -> p t m", t=PACK))
+
+        w2_w = sb([P, 2 * M], U8, "w2_w")
         v_w = [sb([P, HALF], U32, "v_w0")]
         v_s = [sb([P, HALF], U8, "v_s%d" % h) for h in range(2)]
 
         def gather_words(h):
-            nc.vector.tensor_copy(v_w[h][:], tab_w[:].bitcast(U32).indirect(offs_sb[:, h * HALF // 16 : (h + 1) * HALF // 16]))
+            window = tab_w[:].bitcast(U32)
+            nc.vector.tensor_copy(v_w[h][:], window.indirect(picks(offs_sb, h * HALF, (h + 1) * HALF)))
 
-        def gather_scales(h):
-            nc.vector.tensor_copy(v_s[h][:], tab_s[:].indirect(offs_sb[:, h * HALF // 16 : (h + 1) * HALF // 16]))
-
-        gather_scales(0)
-        gather_scales(1)
+        for h in range(2):
+            nc.vector.tensor_copy(v_s[h][:], tab_s[:].indirect(picks(offs_sb, h * HALF, (h + 1) * HALF)))
         gather_words(0)
         w2_s = sb([P, M], U8, "w2_s")
-        nc.vector.tensor_copy(out=w2_s[:].rearrange("p (t m) -> p m t", t=PACK), in_=w2_sraw[:].rearrange("p (m t) -> p m t", t=PACK))
-        v_w.append(keep.tile([P, HALF], U32, name="v_w1", tag="w2_sraw", align_bytes=64))
+        deal(nc.vector.tensor_copy, w2_s[:], w2_sraw[:])
+        v_w.append(sb([P, HALF], U32, "v_w1", tag="w2_sraw"))
         gather_words(1)
-
-        nc.scalar.copy(out=w2_w[:].bitcast(U16).rearrange("p (t m) -> p m t", t=PACK), in_=w2_raw[:].bitcast(U16).rearrange("p (m t) -> p m t", t=PACK))
-
-        def cast_dealt(dst, raw, m0, m1, engine="scalar"):
-            out = dst[:].rearrange("p (t m j) -> p m j t", t=PACK, j=PACK)[:, m0:m1]
-            src = raw.rearrange("p j (m t) -> p m j t", t=PACK)
-            if engine == "scalar":
-                nc.scalar.copy(out=out, in_=src)
-            elif engine == "vector":
-                nc.vector.tensor_copy(out=out, in_=src)
-            else:
-                nc.gpsimd.tensor_scalar(out=out, in0=src, scalar1=1.0, scalar2=0.0, op0=ALU.mult, op1=ALU.add)
-
-        def deal_wc(copy):
-            for a in range(2):
-                copy(
-                    out=wc_w[:, a * N : (a + 1) * N].rearrange("p (t m) -> p m t", t=PACK),
-                    in_=wc_raw[:, a * N : (a + 1) * N].bitcast(U32).rearrange("p (m t) -> p m t", t=PACK),
-                )
-
-        def deal_wc_scales():
-            nc.vector.tensor_copy(out=wc_s[:].rearrange("p (t m) -> p m t", t=PACK), in_=wc_sraw[:].rearrange("p (m t) -> p m t", t=PACK))
-
-        def cast_w1(i, engine="scalar"):
-            cast_dealt(w1_bf[i // 2], w1_raw[i][:], 64 * (i % 2), 64 * (i % 2 + 1), engine)
-
-        def cast_half(dst, raw, i, engine="scalar"):
-            cast_dealt(dst, raw[:, :, 256 * i : 256 * (i + 1)], 64 * i, 64 * (i + 1), engine)
+        deal(nc.scalar.copy, w2_w[:].bitcast(U16), w2_raw[:].bitcast(U16))
 
         def quantised(name):
             return sb([P, 512], U32, name + "_w"), sb([P, 512], U8, name + "_s")
-
-        def quantise(dst, src):
-            nc.vector.quantize_mx(out=dst[0][:].bitcast(FP8X4), scales=dst[1][:], in_=src[:])
 
         w1_bf = [sb([P, PACK * GROUP], BF16, "w1_bf%d" % g) for g in range(2)]
         wa_bf = [sb([P, PACK * GROUP], BF16, "wa_bf%d" % a) for a in range(2)]
@@ -166,6 +159,17 @@ def tile_list_gust_front_page_kernel(
         slope = sb([P, PACK], F32, "slope")
         bias = sb([P, PACK], F32, "bias")
 
+        def round_weight(copy, dst, raw, c0):
+            m0, m1 = c0 // PACK, (c0 + raw.shape[2]) // PACK
+            out = dst[:].rearrange("p (u e m j) -> p u m j e", u=2, e=2, j=PACK)[:, :, m0:m1]
+            copy(out=out, in_=raw.rearrange("p j (m u e) -> p u m j e", u=2, e=2))
+
+        def round_w1(copy, i):
+            round_weight(copy, w1_bf[PIECE * i // GROUP], w1_raw[i][:], PIECE * i % GROUP)
+
+        def quantise(dst, src):
+            nc.vector.quantize_mx(out=dst[0][:].bitcast(FP8X4), scales=dst[1][:], in_=src[:])
+
         def first_stage(words, scales, h, c):
             acc = bank()
             cols = slice(c * CHUNK, (c + 1) * CHUNK)
@@ -177,29 +181,30 @@ def tile_list_gust_front_page_kernel(
             return acc[:].rearrange("p (t n) -> p n t", t=PACK)
 
         def woven(tile, c):
-            return tile[:, c * GROUP : (c + 1) * GROUP].rearrange("p (n t) -> p n t", t=PACK)
+            return tile[:, c * BANK : (c + 1) * BANK].rearrange("p (n t) -> p n t", t=PACK)
 
         def spread(row):
             return row.unsqueeze(1).to_broadcast([P, CHUNK, PACK])
 
-        def make_tanh(h, chunks=range(HALF // CHUNK)):
-            for c in chunks:
+        def make_tanh(h):
+            for c in range(CHUNKS):
                 acc = first_stage(lambda t: w2_w[:, 2 * P * t : 2 * P * (t + 1)].bitcast(FP4X4), w2_s, h, c)
                 nc.scalar.activation(out=woven(tanh_sb[h], c), in_=acc, func=ACT.Tanh)
 
         def make_q(h, chunks, engine, tag):
-            tile = keep.tile([P, len(chunks) * GROUP], BF16, name="q_bf%d%d" % (h, chunks[0]), tag=tag, align_bytes=64)
+            tile = sb([P, len(chunks) * BANK], BF16, "q_bf%d%d" % (h, chunks[0]), tag=tag)
             q_bf[h, chunks[0]] = tile, len(chunks)
             for i, c in enumerate(chunks):
                 engine.tensor_tensor(out=woven(tile, i), in0=woven(tanh_sb[h], c), in1=spread(qgain_sb[:]), op=ALU.mult)
 
-        def quantise_q(h, c):
-            tile, count = q_bf[h, c]
-            cols = slice(c * CHUNK, (c + count) * CHUNK)
-            nc.vector.quantize_mx(out=q_q[h][0][:, cols].bitcast(FP8X4), scales=q_q[h][1][:, cols], in_=tile[:])
+        def quantise_q(h):
+            for c in (GPSIMD_CHUNKS[0], VECTOR_CHUNKS[0]):
+                tile, count = q_bf[h, c]
+                cols = slice(c * CHUNK, (c + count) * CHUNK)
+                nc.vector.quantize_mx(out=q_q[h][0][:, cols].bitcast(FP8X4), scales=q_q[h][1][:, cols], in_=tile[:])
 
-        def make_h(g, h, chunks=range(HALF // CHUNK)):
-            for c in chunks:
+        def make_h(g, h):
+            for c in range(CHUNKS):
                 acc = first_stage(lambda t: w1_q[g][0][:, P * t : P * (t + 1)].bitcast(FP8X4), w1_q[g][1], h, c)
                 nc.vector.tensor_tensor(out=woven(h_bf[g][h], c), in0=acc, in1=spread(b1_sb[:, g, :]), op=ALU.add)
 
@@ -212,7 +217,8 @@ def tile_list_gust_front_page_kernel(
         def make_d(t, h):
             acc = bank()
             for a in range(2):
-                second_pass(acc, wc_w[:, a * N + t * P : a * N + (t + 1) * P], wc_s[4 * a :, t * P : (t + 1) * P], h_q[a][h], a == 0, a == 1)
+                words = wc_w[:, a * N + t * P : a * N + (t + 1) * P]
+                second_pass(acc, words, wc_s[4 * a :, t * P : (t + 1) * P], h_q[a][h], a == 0, a == 1)
             nc.scalar.copy(out=d_sb[t][:, h * HALF : (h + 1) * HALF], in_=acc[:])
 
         def make_e(t, h):
@@ -228,49 +234,51 @@ def tile_list_gust_front_page_kernel(
                 accum_out=(top0 if h == 0 else top)[:, col],
             )
 
-        cast_w1(0)
-        cast_dealt(w1_bf[0], w1_raw[1][:, :, :128], 64, 96)
-        cast_dealt(w1_bf[0], w1_raw[1][:, :, 128:], 96, 128, "vector")
+        round_w1(nc.scalar.copy, 0)
+        round_w1(nc.vector.tensor_copy, 1)
         make_tanh(0)
         quantise(w1_q[0], w1_bf[0])
-        make_q(0, [0, 1, 2], nc.gpsimd, "w1_bf0")
+        make_q(0, GPSIMD_CHUNKS, nc.gpsimd, "w1_bf0")
         make_h(0, 0)
         make_h(0, 1)
-        cast_w1(2)
-        cast_w1(3)
+        round_w1(nc.scalar.copy, 2)
+        round_w1(nc.scalar.copy, 3)
         make_tanh(1)
-        deal_wc(nc.scalar.copy)
+        for a in range(2):
+            nc.scalar.copy(
+                out=wc_w[:, a * N : (a + 1) * N].rearrange("p (u e m) -> p u m e", u=2, e=2),
+                in_=wc_raw[:, a * N : (a + 1) * N].bitcast(U32).rearrange("p (m u e) -> p u m e", u=2, e=2),
+            )
         quantise(w1_q[1], w1_bf[1])
-        deal_wc_scales()
+        deal(nc.vector.tensor_copy, wc_s[:], wc_sraw[:])
         quantise(h_q[0][0], h_bf[0][0])
         quantise(h_q[0][1], h_bf[0][1])
-        make_q(1, [0, 1, 2], nc.gpsimd, "h_bf01")
-        h_bf[1].append(keep.tile([P, PACK * HALF], BF16, name="h_bf10", tag="wc_sraw", align_bytes=64))
+        make_q(1, GPSIMD_CHUNKS, nc.gpsimd, "h_bf01")
+        h_bf[1].append(sb([P, PACK * HALF], BF16, "h_bf10", tag="wc_sraw"))
         h_bf[1].append(sb([P, PACK * HALF], BF16, "h_bf11"))
         make_h(1, 0)
         make_h(1, 1)
+
         for a in range(2):
-            for i in range(2):
-                cast_half(wa_bf[a], wa_raw[a], i)
-        for i in range(2):
-            cast_half(wb_bf, wb_raw, i)
+            for c0 in range(0, N, PIECE):
+                round_weight(nc.scalar.copy, wa_bf[a], wa_raw[a][:, :, c0 : c0 + PIECE], c0)
         quantise(h_q[1][0], h_bf[1][0])
         quantise(h_q[1][1], h_bf[1][1])
         for h in range(2):
             for t in range(PACK):
                 make_d(t, h)
+        round_weight(nc.vector.tensor_copy, wb_bf, wb_raw[:], 0)
         quantise(wa_q[0], wa_bf[0])
-        make_q(0, [3], nc.vector, "qc")
+        make_q(0, VECTOR_CHUNKS, nc.vector, None)
         quantise(wa_q[1], wa_bf[1])
-        make_q(1, [3], nc.vector, "qd")
-        quantise_q(0, 0)
-        quantise_q(0, 3)
+        make_q(1, VECTOR_CHUNKS, nc.vector, None)
+        quantise_q(0)
         quantise(wb_q, wb_bf)
-        quantise_q(1, 0)
-        quantise_q(1, 3)
-        nc.vector.scalar_tensor_tensor(out=slope[:], in0=steep_sb[:], scalar=-1.0, in1=share_sb[:], op0=ALU.mult, op1=ALU.mult)
+        quantise_q(1)
+        nc.vector.scalar_tensor_tensor(
+            out=slope[:], in0=steep_sb[:], scalar=-1.0, in1=share_sb[:], op0=ALU.mult, op1=ALU.mult
+        )
 
-        PART = PICKS // 2
         gate = sb([P, PACK, PICKS], F32, "gate")
         summed = sb([P, PACK, PICKS], F32, "summed")
         y = sb([P, PACK, PICKS], F32, "y")
@@ -280,51 +288,63 @@ def tile_list_gust_front_page_kernel(
         out_rows = out_0.rearrange("(p t) c -> p t c", t=PACK)
         out_words = out_1[0].rearrange("p m t -> p (m t)").bitcast(I32)
 
-        def scores(t):
-            col = slice(t, t + 1)
-            make_e(t, 0)
-            make_e(t, 1)
-            nc.vector.tensor_tensor(out=bias[:, col], in0=top[:, col], in1=slope[:, col], op=ALU.mult)
-
         def look(t, c0, c1):
             col = slice(t, t + 1)
             nc.scalar.activation(
-                out=gate[:, t, c0:c1], in_=e_sb[t][:].indirect(pos1_sb[:, c0 // 16 : c1 // 16]),
+                out=gate[:, t, c0:c1], in_=e_sb[t][:].indirect(picks(pos1_sb, c0, c1)),
                 func=ACT.Sigmoid, bias=bias[:, col], scale=steep_sb[:, col],
             )
 
-        def combine(t, c0, c1, last=False):
+        def combine(t, c0, c1):
             nc.vector.tensor_tensor(out=gate[:, t, c0:c1], in0=gate[:, t, c0:c1], in1=mat_sb[:, t, c0:c1], op=ALU.mult)
-            nc.vector.tensor_tensor(out=summed[:, t, c0:c1], in0=d_sb[t][:].indirect(pos2_sb[:, c0 // 16 : c1 // 16]), in1=gate[:, t, c0:c1], op=ALU.add)
-            if last:
-                nc.vector.tensor_scalar(out=y[:, t, c0:c1], in0=summed[:, t, c0:c1], scalar1=gain_sb[:, t : t + 1], scalar2=None, op0=ALU.mult)
-            else:
-                nc.scalar.activation(out=y[:, t, c0:c1], in_=summed[:, t, c0:c1], func=ACT.Copy, scale=gain_sb[:, t : t + 1])
+            nc.vector.tensor_tensor(
+                out=summed[:, t, c0:c1], in0=d_sb[t][:].indirect(picks(pos2_sb, c0, c1)), in1=gate[:, t, c0:c1], op=ALU.add
+            )
+
+        def store(t, c0, c1):
             nc.sync.dma_start(out=out_rows[:, t, c0:c1], in_=y[:, t, c0:c1])
 
-        def planes(c, split):
+        def finish(t, c0, c1):
+            combine(t, c0, c1)
+            nc.scalar.activation(out=y[:, t, c0:c1], in_=summed[:, t, c0:c1], func=ACT.Copy, scale=gain_sb[:, t : t + 1])
+            store(t, c0, c1)
+
+        def weave_y(copy, c, runs):
             cols = slice(c * PART, (c + 1) * PART)
-            woven_y = y_bf[c][:].rearrange("p (c i t) -> p c t i", i=4, t=PACK)
-            rows_y = y[:, :, cols].rearrange("p t (c i) -> p c t i", i=4)
-            if split:
-                nc.vector.tensor_copy(out=woven_y[:, :split], in_=rows_y[:, :split])
-            nc.scalar.copy(out=woven_y[:, split:], in_=rows_y[:, split:])
+            copy(
+                out=y_bf[c][:].rearrange("p (r i t) -> p r t i", i=4, t=PACK)[:, runs],
+                in_=y[:, :, cols].rearrange("p t (r i) -> p r t i", i=4)[:, runs],
+            )
+
+        def planes(c):
+            cols = slice(c * PART, (c + 1) * PART)
             nc.vector.quantize_mx(out=y_w[c][:].bitcast(FP8X4), scales=y_s[:, cols], in_=y_bf[c][:])
             nc.sync.dma_start(out=out_words[:, cols], in_=y_w[c][:].bitcast(I32))
 
+        whole, parted = range(PACK // 2), range(PACK // 2, PACK)
         for t in range(PACK):
-            scores(t)
-            look(t, 0, PICKS if t < 2 else PART)
-        look(2, PART, PICKS)
-        look(3, PART, PICKS)
-        combine(0, 0, PICKS)
-        combine(1, 0, PICKS)
-        combine(2, 0, PART)
-        combine(3, 0, PART)
-        planes(0, 0)
-        combine(2, PART, PICKS)
-        combine(3, PART, PICKS, last=True)
-        planes(1, 36)
+            make_e(t, 0)
+            make_e(t, 1)
+            nc.vector.tensor_tensor(out=bias[:, t : t + 1], in0=top[:, t : t + 1], in1=slope[:, t : t + 1], op=ALU.mult)
+            look(t, 0, PICKS if t in whole else PART)
+        for t in parted:
+            look(t, PART, PICKS)
+        for t in whole:
+            finish(t, 0, PICKS)
+        for t in parted:
+            finish(t, 0, PART)
+        weave_y(nc.scalar.copy, 0, slice(None))
+        planes(0)
+        finish(parted[0], PART, PICKS)
+        last = parted[1]
+        combine(last, PART, PICKS)
+        nc.vector.tensor_scalar(
+            out=y[:, last, PART:], in0=summed[:, last, PART:], scalar1=gain_sb[:, last : last + 1], scalar2=None, op0=ALU.mult
+        )
+        store(last, PART, PICKS)
+        weave_y(nc.vector.tensor_copy, 1, slice(None, VECTOR_RUNS))
+        weave_y(nc.scalar.copy, 1, slice(VECTOR_RUNS, None))
+        planes(1)
         for q in range(QUADS):
             queue = nc.scalar if q % 2 else nc.sync
             queue.dma_start(out=out_2[0, 4 * q : 4 * q + 4, :].bitcast(I32), in_=y_s[32 * q : 32 * q + 4, :].bitcast(I32))

from contextlib import ExitStack

import concourse.mybir as mybir

K, T, S, H, M, N, PICKS = 512, 2048, 1024, 1024, 512, 512, 512
FLOPS = 2 * S * (K * H + K * M + H * N + M * N + H * N)

F32 = mybir.dt.float32
BF16 = mybir.dt.bfloat16
I32 = mybir.dt.int32
U32 = mybir.dt.uint32
U16 = mybir.dt.uint16
U8 = mybir.dt.uint8
FP8X4 = mybir.dt.float8_e4m3fn_x4
FP4X4 = mybir.dt.float4_e2m1fn_x4
ACT = mybir.ActivationFunctionType
ALU = mybir.AluOpType

P = 128
PACK = 4
GROUP = P * PACK
BANK = 512
BANKS = 8
HALF = S // 2
CHUNK = BANK // PACK
CHUNKS = HALF // CHUNK
PIECE = 256
QUADS = 4
LIST = 16
PART = PICKS // 2
GPSIMD_CHUNKS = [0, 1, 2]
VECTOR_CHUNKS = [3]
VECTOR_RUNS = 36


def tile_list_gust_front_page_kernel(
    tc, tab_words, tab_scales, offs, pos1, pos2, w1, b1, w2_words, w2_scales, qgain, wa, wb,
    wc_words, wc_scales, steep, share, mat, gain, out_0, out_1, out_2,
):
    nc = tc.nc
    with ExitStack() as ctx:
        keep = ctx.enter_context(tc.tile_pool(name="keep", bufs=1))
        psum = ctx.enter_context(tc.psum_pool(name="psum", bufs=BANKS))

        def sb(shape, dtype, name, tag=None):
            return keep.tile(shape, dtype, name=name, tag=tag or name, align_bytes=64)

        def bank():
            return psum.tile([P, BANK], F32, name="bank")

        offs_sb = keep.tile([P, S // LIST], U16, name="offs_sb")
        pos1_sb = keep.tile([P, PICKS // LIST], U16, name="pos1_sb")
        pos2_sb = keep.tile([P, PICKS // LIST], U16, name="pos2_sb")

        tab_w = sb([P, T], I32, "tab_w")
        tab_s = sb([P, T], U8, "tab_s")
        w2_raw = sb([P, 2 * M], U8, "w2_raw")
        w2_sraw = sb([P, M], U8, "w2_sraw")
        wc_raw = sb([P, 2 * N], I32, "wc_raw")
        wc_sraw = sb([P, N], U8, "wc_sraw")
        w1_raw = [sb([P, PACK, PIECE], F32, "w1_raw%d" % i) for i in range(H // PIECE)]
        wa_raw = [sb([P, PACK, N], F32, "wa_raw%d" % a) for a in range(2)]
        wb_raw = sb([P, PACK, N], F32, "wb_raw")
        mat_sb = sb([P, PACK, PICKS], F32, "mat_sb")
        b1_sb = sb([P, 2, PACK], F32, "b1_sb")
        qgain_sb = sb([P, PACK], F32, "qgain_sb")
        steep_sb = sb([P, PACK], F32, "steep_sb")
        share_sb = sb([P, PACK], F32, "share_sb")
        gain_sb = sb([P, PACK], F32, "gain_sb")

        nc.gpsimd.memset(tab_s[:].bitcast(I32), 0)
        nc.gpsimd.memset(w2_sraw[:].bitcast(I32), 0)
        nc.gpsimd.memset(wc_sraw[:].bitcast(I32), 0)

        def load_vector(vec_sb, vec):
            nc.sync.dma_start(out=vec_sb[:], in_=vec.rearrange("(p t) -> p t", t=PACK))

        def load_rows(raw, rows):
            nc.sync.dma_start(out=raw[:], in_=rows.rearrange("(p j) c -> p j c", j=PACK))

        def load_scales(tile, rows_of):
            for q in range(QUADS):
                rows = rows_of(slice(4 * q, 4 * q + 4))
                count = 4 * (rows.shape[0] if rows.ndim == 3 else 1)
                nc.sync.dma_start(out=tile[32 * q : 32 * q + count, :].bitcast(I32), in_=rows.bitcast(I32))

        def load_w1(i):
            load_rows(w1_raw[i], w1[:, PIECE * i : PIECE * (i + 1)])

        nc.sync.dma_start(offs_sb[:], offs)
        nc.sync.dma_start(pos1_sb[:], pos1)
        nc.sync.dma_start(pos2_sb[:], pos2)
        load_scales(tab_s, lambda rows: tab_scales[0, rows, :])
        nc.sync.dma_start(out=tab_w[:], in_=tab_words[0].rearrange("p t i -> p (t i)").bitcast(I32))
        nc.sync.dma_start(out=w2_raw[:].bitcast(I32), in_=w2_words[0].bitcast(I32))
        load_w1(0)
        load_scales(w2_sraw, lambda rows: w2_scales[0, rows, :])
        load_w1(1)
        load_w1(2)
        nc.sync.dma_start(out=b1_sb[:], in_=b1.rearrange("(g p t) -> p g t", g=2, t=PACK))
        load_vector(qgain_sb, qgain)
        load_w1(3)
        nc.sync.dma_start(
            out=wc_raw[:].rearrange("p (a c) -> p a c", a=2),
            in_=wc_words.rearrange("a p c i -> p a (c i)").bitcast(I32),
        )
        load_scales(wc_sraw, lambda rows: wc_scales[:, rows, :])
        for a in range(2):
            load_rows(wa_raw[a], wa[GROUP * a : GROUP * (a + 1), :])
        load_rows(wb_raw, wb)
        load_vector(steep_sb, steep)
        load_vector(share_sb, share)
        load_rows(mat_sb, mat)
        load_vector(gain_sb, gain)

        def picks(list_sb, j0, j1):
            return list_sb[:, j0 // LIST : j1 // LIST]

        def deal(copy, dst, src):
            copy(out=dst.rearrange("p (t m) -> p t m", t=PACK), in_=src.rearrange("p (m t) -> p t m", t=PACK))

        w2_w = sb([P, 2 * M], U8, "w2_w")
        v_w = [sb([P, HALF], U32, "v_w0")]
        v_s = [sb([P, HALF], U8, "v_s%d" % h) for h in range(2)]

        def gather_words(h):
            window = tab_w[:].bitcast(U32)
            nc.vector.tensor_copy(v_w[h][:], window.indirect(picks(offs_sb, h * HALF, (h + 1) * HALF)))

        for h in range(2):
            nc.vector.tensor_copy(v_s[h][:], tab_s[:].indirect(picks(offs_sb, h * HALF, (h + 1) * HALF)))
        gather_words(0)
        w2_s = sb([P, M], U8, "w2_s")
        deal(nc.vector.tensor_copy, w2_s[:], w2_sraw[:])
        v_w.append(sb([P, HALF], U32, "v_w1", tag="w2_sraw"))
        gather_words(1)
        deal(nc.scalar.copy, w2_w[:].bitcast(U16), w2_raw[:].bitcast(U16))

        def quantised(name):
            return sb([P, 512], U32, name + "_w"), sb([P, 512], U8, name + "_s")

        w1_bf = [sb([P, PACK * GROUP], BF16, "w1_bf%d" % g) for g in range(2)]
        wa_bf = [sb([P, PACK * GROUP], BF16, "wa_bf%d" % a) for a in range(2)]
        wb_bf = sb([P, PACK * GROUP], BF16, "wb_bf")
        w1_q = [quantised("w1_q%d" % g) for g in range(2)]
        wa_q = [quantised("wa_q%d" % a) for a in range(2)]
        wb_q = quantised("wb_q")
        h_bf = [[sb([P, PACK * HALF], BF16, "h_bf0%d" % h) for h in range(2)], []]
        h_q = [[quantised("h_q%d%d" % (g, h)) for h in range(2)] for g in range(2)]
        tanh_sb = [sb([P, PACK * HALF], F32, "tanh%d" % h) for h in range(2)]
        q_bf = {}
        q_q = [quantised("q_q%d" % h) for h in range(2)]
        wc_w = sb([P, 2 * N], U32, "wc_w")
        wc_s = sb([P, N], U8, "wc_s")
        e_sb = [sb([P, S], F32, "e%d" % t) for t in range(PACK)]
        d_sb = [sb([P, S], F32, "d%d" % t) for t in range(PACK)]
        top0 = sb([P, PACK], F32, "top0")
        top = sb([P, PACK], F32, "top")
        slope = sb([P, PACK], F32, "slope")
        bias = sb([P, PACK], F32, "bias")

        def round_weight(copy, dst, raw, c0):
            m0, m1 = c0 // PACK, (c0 + raw.shape[2]) // PACK
            out = dst[:].rearrange("p (u e m j) -> p u m j e", u=2, e=2, j=PACK)[:, :, m0:m1]
            copy(out=out, in_=raw.rearrange("p j (m u e) -> p u m j e", u=2, e=2))

        def round_w1(copy, i):
            round_weight(copy, w1_bf[PIECE * i // GROUP], w1_raw[i][:], PIECE * i % GROUP)

        def quantise(dst, src):
            nc.vector.quantize_mx(out=dst[0][:].bitcast(FP8X4), scales=dst[1][:], in_=src[:])

        def first_stage(words, scales, h, c):
            acc = bank()
            cols = slice(c * CHUNK, (c + 1) * CHUNK)
            for t in range(PACK):
                nc.tensor.matmul_mx(
                    out=acc[:, t * CHUNK : (t + 1) * CHUNK], lhsT=words(t), lhsT_scale=scales[:, t * P : (t + 1) * P],
                    rhs=v_w[h][:, cols].bitcast(FP8X4), rhs_scale=v_s[h][:, cols], start=True, stop=True,
                )
            return acc[:].rearrange("p (t n) -> p n t", t=PACK)

        def woven(tile, c):
            return tile[:, c * BANK : (c + 1) * BANK].rearrange("p (n t) -> p n t", t=PACK)

        def spread(row):
            return row.unsqueeze(1).to_broadcast([P, CHUNK, PACK])

        def make_tanh(h):
            for c in range(CHUNKS):
                acc = first_stage(lambda t: w2_w[:, 2 * P * t : 2 * P * (t + 1)].bitcast(FP4X4), w2_s, h, c)
                nc.scalar.activation(out=woven(tanh_sb[h], c), in_=acc, func=ACT.Tanh)

        def make_q(h, chunks, engine, tag):
            tile = sb([P, len(chunks) * BANK], BF16, "q_bf%d%d" % (h, chunks[0]), tag=tag)
            q_bf[h, chunks[0]] = tile, len(chunks)
            for i, c in enumerate(chunks):
                engine.tensor_tensor(out=woven(tile, i), in0=woven(tanh_sb[h], c), in1=spread(qgain_sb[:]), op=ALU.mult)

        def quantise_q(h):
            for c in (GPSIMD_CHUNKS[0], VECTOR_CHUNKS[0]):
                tile, count = q_bf[h, c]
                cols = slice(c * CHUNK, (c + count) * CHUNK)
                nc.vector.quantize_mx(out=q_q[h][0][:, cols].bitcast(FP8X4), scales=q_q[h][1][:, cols], in_=tile[:])

        def make_h(g, h):
            for c in range(CHUNKS):
                acc = first_stage(lambda t: w1_q[g][0][:, P * t : P * (t + 1)].bitcast(FP8X4), w1_q[g][1], h, c)
                nc.vector.tensor_tensor(out=woven(h_bf[g][h], c), in0=acc, in1=spread(b1_sb[:, g, :]), op=ALU.add)

        def second_pass(acc, words, scales, moving, start, stop):
            nc.tensor.matmul_mx(
                out=acc[:], lhsT=words.bitcast(FP8X4), lhsT_scale=scales,
                rhs=moving[0][:].bitcast(FP8X4), rhs_scale=moving[1][:], start=start, stop=stop,
            )

        def make_d(t, h):
            acc = bank()
            for a in range(2):
                words = wc_w[:, a * N + t * P : a * N + (t + 1) * P]
                second_pass(acc, words, wc_s[4 * a :, t * P : (t + 1) * P], h_q[a][h], a == 0, a == 1)
            nc.scalar.copy(out=d_sb[t][:, h * HALF : (h + 1) * HALF], in_=acc[:])

        def make_e(t, h):
            acc = bank()
            cols = slice(t * P, (t + 1) * P)
            col = slice(t, t + 1)
            for a in range(2):
                second_pass(acc, wa_q[a][0][:, cols], wa_q[a][1][:, cols], h_q[a][h], a == 0, False)
            second_pass(acc, wb_q[0][:, cols], wb_q[1][:, cols], q_q[h], False, True)
            nc.vector.tensor_scalar(
                out=e_sb[t][:, h * HALF : (h + 1) * HALF], in0=acc[:], scalar1=1.0,
                scalar2=(None if h == 0 else top0[:, col]), op0=ALU.mult, op1=ALU.max,
                accum_out=(top0 if h == 0 else top)[:, col],
            )

        round_w1(nc.scalar.copy, 0)
        round_w1(nc.vector.tensor_copy, 1)
        make_tanh(0)
        quantise(w1_q[0], w1_bf[0])
        make_q(0, GPSIMD_CHUNKS, nc.gpsimd, "w1_bf0")
        make_h(0, 0)
        make_h(0, 1)
        round_w1(nc.scalar.copy, 2)
        round_w1(nc.scalar.copy, 3)
        make_tanh(1)
        for a in range(2):
            nc.scalar.copy(
                out=wc_w[:, a * N : (a + 1) * N].rearrange("p (u e m) -> p u m e", u=2, e=2),
                in_=wc_raw[:, a * N : (a + 1) * N].bitcast(U32).rearrange("p (m u e) -> p u m e", u=2, e=2),
            )
        quantise(w1_q[1], w1_bf[1])
        deal(nc.vector.tensor_copy, wc_s[:], wc_sraw[:])
        quantise(h_q[0][0], h_bf[0][0])
        quantise(h_q[0][1], h_bf[0][1])
        make_q(1, GPSIMD_CHUNKS, nc.gpsimd, "h_bf01")
        h_bf[1].append(sb([P, PACK * HALF], BF16, "h_bf10", tag="wc_sraw"))
        h_bf[1].append(sb([P, PACK * HALF], BF16, "h_bf11"))
        make_h(1, 0)
        make_h(1, 1)

        for a in range(2):
            for c0 in range(0, N, PIECE):
                round_weight(nc.scalar.copy, wa_bf[a], wa_raw[a][:, :, c0 : c0 + PIECE], c0)
        quantise(h_q[1][0], h_bf[1][0])
        quantise(h_q[1][1], h_bf[1][1])
        for h in range(2):
            for t in range(PACK):
                make_d(t, h)
        round_weight(nc.vector.tensor_copy, wb_bf, wb_raw[:], 0)
        quantise(wa_q[0], wa_bf[0])
        make_q(0, VECTOR_CHUNKS, nc.vector, None)
        quantise(wa_q[1], wa_bf[1])
        make_q(1, VECTOR_CHUNKS, nc.vector, None)
        quantise_q(0)
        quantise(wb_q, wb_bf)
        quantise_q(1)
        nc.vector.scalar_tensor_tensor(
            out=slope[:], in0=steep_sb[:], scalar=-1.0, in1=share_sb[:], op0=ALU.mult, op1=ALU.mult
        )

        gate = sb([P, PACK, PICKS], F32, "gate")
        summed = sb([P, PACK, PICKS], F32, "summed")
        y = sb([P, PACK, PICKS], F32, "y")
        y_bf = [sb([P, PACK * PART], BF16, "y_bf%d" % c) for c in range(2)]
        y_w = [sb([P, PART], U32, "y_w%d" % c) for c in range(2)]
        y_s = sb([P, PICKS], U8, "y_s")
        out_rows = out_0.rearrange("(p t) c -> p t c", t=PACK)
        out_words = out_1[0].rearrange("p m t -> p (m t)").bitcast(I32)

        def look(t, c0, c1):
            col = slice(t, t + 1)
            nc.scalar.activation(
                out=gate[:, t, c0:c1], in_=e_sb[t][:].indirect(picks(pos1_sb, c0, c1)),
                func=ACT.Sigmoid, bias=bias[:, col], scale=steep_sb[:, col],
            )

        def combine(t, c0, c1):
            nc.vector.tensor_tensor(out=gate[:, t, c0:c1], in0=gate[:, t, c0:c1], in1=mat_sb[:, t, c0:c1], op=ALU.mult)
            nc.vector.tensor_tensor(
                out=summed[:, t, c0:c1], in0=d_sb[t][:].indirect(picks(pos2_sb, c0, c1)), in1=gate[:, t, c0:c1], op=ALU.add
            )

        def store(t, c0, c1):
            nc.sync.dma_start(out=out_rows[:, t, c0:c1], in_=y[:, t, c0:c1])

        def finish(t, c0, c1):
            combine(t, c0, c1)
            nc.scalar.activation(out=y[:, t, c0:c1], in_=summed[:, t, c0:c1], func=ACT.Copy, scale=gain_sb[:, t : t + 1])
            store(t, c0, c1)

        def weave_y(copy, c, runs):
            cols = slice(c * PART, (c + 1) * PART)
            copy(
                out=y_bf[c][:].rearrange("p (r i t) -> p r t i", i=4, t=PACK)[:, runs],
                in_=y[:, :, cols].rearrange("p t (r i) -> p r t i", i=4)[:, runs],
            )

        def planes(c):
            cols = slice(c * PART, (c + 1) * PART)
            nc.vector.quantize_mx(out=y_w[c][:].bitcast(FP8X4), scales=y_s[:, cols], in_=y_bf[c][:])
            nc.sync.dma_start(out=out_words[:, cols], in_=y_w[c][:].bitcast(I32))

        whole, parted = range(PACK // 2), range(PACK // 2, PACK)
        for t in range(PACK):
            make_e(t, 0)
            make_e(t, 1)
            nc.vector.tensor_tensor(out=bias[:, t : t + 1], in0=top[:, t : t + 1], in1=slope[:, t : t + 1], op=ALU.mult)
            look(t, 0, PICKS if t in whole else PART)
        for t in parted:
            look(t, PART, PICKS)
        for t in whole:
            finish(t, 0, PICKS)
        for t in parted:
            finish(t, 0, PART)
        weave_y(nc.scalar.copy, 0, slice(None))
        planes(0)
        finish(parted[0], PART, PICKS)
        last = parted[1]
        combine(last, PART, PICKS)
        nc.vector.tensor_scalar(
            out=y[:, last, PART:], in0=summed[:, last, PART:], scalar1=gain_sb[:, last : last + 1], scalar2=None, op0=ALU.mult
        )
        store(last, PART, PICKS)
        weave_y(nc.vector.tensor_copy, 1, slice(None, VECTOR_RUNS))
        weave_y(nc.scalar.copy, 1, slice(VECTOR_RUNS, None))
        planes(1)
        for q in range(QUADS):
            queue = nc.scalar if q % 2 else nc.sync
            queue.dma_start(out=out_2[0, 4 * q : 4 * q + 4, :].bitcast(I32), in_=y_s[32 * q : 32 * q + 4, :].bitcast(I32))
